import numpy as np, ml_dtypes
CORES = [40,64,80,88,96,104,120,144]
N = 8
import mx_ref
BF = ml_dtypes.bfloat16
def pick(q, e):
    c = np.concatenate([q[0].reshape(128, -1, 4), np.zeros((128, 1, 4), np.uint8)], axis=1); s = np.concatenate([q[1], np.ones((16, 1), np.uint8)], axis=1)
    return (np.ascontiguousarray(c[:, e].reshape(128, -1)), np.ascontiguousarray(s[:, e]))
def join(*qs):
    return (np.concatenate([q[0] for q in qs], axis=1), np.concatenate([q[1] for q in qs], axis=1))
def put(q, e, v):
    c, s = q[0].reshape(128, -1, 4).copy(), q[1].copy(); c[:, e] = v[0].reshape(128, -1, 4); s[:, e] = v[1]
    return (c.reshape(128, -1), s)
def pk(c, s):
    return (np.ascontiguousarray(c), mx_ref.live(s))
def emit(q):
    return q[0], q[1]
def decode(q):
    o = []
    for b in range(4):
        e = np.zeros((128, 128, 4), np.float32); e[np.arange(128), np.arange(128), b] = 1
        o.append(mx_ref.matmul(mx_ref.quantize(e.reshape(128, 512).astype(BF)), q))
    return np.stack(o, axis=2).reshape(128, -1)
def cols(t, e):
    v = np.concatenate([t.reshape(128, -1, 4), np.zeros((128, 1, 4), BF)], axis=1)
    return np.ascontiguousarray(v[:, e]).reshape(128, -1)
def cut(t, i, w=512):
    return t[:, w * i:w * i + w]
def f(rng, *shape):
    return mx_ref.flush((rng.standard_normal(shape, dtype=np.float32) * np.exp2(rng.integers(-2, 3, shape[:-1] + (1,)))).astype(BF))
def wide(rng, *shape, cols=0):
    v = rng.standard_normal(shape, dtype=np.float32) * np.exp2(rng.integers(-12, 13, shape)).astype(np.float32)
    if cols: v *= np.repeat(np.exp2(rng.integers(-cols, cols + 1, shape[:-2] + (1, shape[-1] // 4))) * (rng.random(shape[:-2] + (1, shape[-1] // 4)) > 0.0625), 4, axis=-1).astype(np.float32)
    return mx_ref.flush(v.astype(BF))
C, T, R, O = 128, 32, 3, 1
def trim(v):
    v = v.astype(np.float32)
    v[np.abs(v) < np.float32(2.0 ** -14)] = 0
    return v.astype(BF)
def given(rng, u, x):
    return {"kb": np.stack([trim(u.reshape(128, 4 * C))] * N), "x": trim(x.reshape(N, 128, 4 * R * T)), "w": f(rng, N, 128, 512 * O)}
def sturdy(rng, n):
    return (1 + rng.random((128, n, 4))) * rng.choice([-1.0, 1.0], (128, n, 4)) * np.exp2(rng.integers(-1, 2, (128, 1, 1)))
def kept(v):
    m, e = np.frexp(v)
    return np.ldexp(np.trunc(m * 8) * 0.125, e)
def near(rng, u, e):
    return u[:, e] + 0.5 * sturdy(rng, len(e))
def setup_inputs(rng):
    return given(rng, f(rng, 128, 4 * C), f(rng, N, 128, 4 * R * T))
def setup_inputs_both(rng):
    u, x, new = kept(sturdy(rng, C)), np.zeros((N, 128, R, T, 4)), np.zeros((N, C), bool)
    for b in range(R):
        for j, r in enumerate(rng.permutation([v for v in range(N) if v < v ^ (1 << b)])):
            p, e = r ^ (1 << b), rng.permutation(C)
            if j % 2: e = e[np.argsort(new[r, e] | ~new[p, e], kind="stable")]
            t = e[T:2 * T] if j % 2 else rng.permutation(e[:T])
            x[r, :, b] = near(rng, u, e[:T])
            x[r, :, b, :T // 4] = u[:, e[:T // 4]]
            x[p, :, b] = near(rng, u, t)
            for s in (r, p):
                new[s, e[:T]] = True
                new[s, t] = True
    return given(rng, u, x)
def setup_inputs_few(rng):
    u, x, four = sturdy(rng, C), np.zeros((N, 128, R, T, 4)), rng.permutation(C)[:4]
    for b in range(R):
        for j, r in enumerate(rng.permutation([v for v in range(N) if v < v ^ (1 << b)])):
            a = rng.permutation(four)[:2]
            for s, c in ((r, a[0]), (r ^ (1 << b), a[j % 2])):
                x[s, :, b] = near(rng, u, np.full(T, c)) * np.exp2(rng.integers(-1, 2, (1, T, 1)))
    return given(rng, u, x)
def setup_inputs_ties(rng):
    u = np.abs(cols(f(rng, 128, 4 * (C // 4)), rng.permutation(np.arange(C) % (C // 4))).astype(np.float32))
    x = np.abs(f(rng, N, 128, 4 * R * T).astype(np.float32)).reshape(N, 128, R, T, 4)
    for r in range(N):
        for b in range(R):
            x[r, :, b] *= (1 - 2 * (rng.permutation(T) % 2)).astype(np.float32)[:, None]
            x[r, :, b, int(rng.integers(0, T))] = 0
    return given(rng, u * np.float32(2.0 ** 18), x * np.float32(2.0 ** 18))
def setup_inputs_drift(rng):
    top = (rng.permutation(128) < 64)[:, None, None]
    u, z, x = sturdy(rng, C) * top, sturdy(rng, 8) * ~top, np.zeros((N, 128, R, T, 4))
    e = rng.permutation(C)
    for r in range(N):
        for b in range(R):
            t = rng.permutation(e[:C // 2] if b == 0 else e[C // 2:])[:T]
            x[r, :, b] = near(rng, u, t) * top + 8 * z[:, rng.permutation(np.arange(T) % 8)]
    return given(rng, u, x)
def setup_inputs_spread(rng):
    d = given(rng, wide(rng, 128, 4 * C, cols=2), wide(rng, N, 128, 4 * R * T, cols=6))
    d["kb"][:, :, :4] = BF(-0.0)
    for r in range(N):
        for b in range(R):
            i = 4 * (b * T + int(rng.integers(0, T)))
            d["x"][r, :, i:i + 4] = BF(0.0)
    return d
def check_inputs(d):
    b = []
    for n, lo, hi in (("kb", -14, 24), ("x", -14, 24), ("w", -30, 30)):
        v = np.abs(d[n].astype(np.float32))
        if not (np.isfinite(v).all() and ((v == 0) | (v >= 2.0 ** lo) & (v <= 2.0 ** hi)).all()): b.append("a value of " + n)
    if (d["kb"].astype(np.float32) != d["kb"][:1].astype(np.float32)).any(): b.append("kb isn't the same on all ranks")
    return b
def numbers(k, e):
    return decode(pick(k, np.concatenate([e, np.full(-len(e) % 4, -1)]))).reshape(128, -1, 4)[:, :len(e)]
def anew(k, e, v):
    t = np.zeros((128, len(e) + -len(e) % 4, 4), np.float32)
    t[:, :len(e)] = v
    return put(k, e, pick(mx_ref.quantize(t.reshape(128, -1).astype(BF)), np.arange(len(e))))
def reference(kb, x, w):
    k = join(*[mx_ref.quantize(np.ascontiguousarray(kb[r])) for r in range(N)])
    q = join(*[mx_ref.quantize(np.ascontiguousarray(x[r])) for r in range(N)])
    dx = decode(q).reshape(128, N, R, T, 4)
    ch = np.zeros((N, R, T), np.float32)
    for b in range(R):
        won, e, t = np.zeros((N, C), bool), [], []
        for r in range(N):
            v = pick(q, (r * R + b) * T + np.arange(T))
            s = np.concatenate([mx_ref.matmul(pick(k, C * r + 128 * m + np.arange(128)), v) for m in range(C // 128)])
            win = np.argmax(s + np.float32(0), axis=0)
            u, i = np.unique(win, return_index=True)
            won[r, u] = True
            e.append(C * r + u)
            t.append(dx[:, r, b, i])
            ch[r, b] = win
        e = np.concatenate(e)
        k = anew(k, e, np.float32(0.75) * numbers(k, e) + np.float32(0.25) * np.concatenate(t, axis=1))
        src, low, high = np.arange(N * C).reshape(N, C), [], []
        for r in range(N):
            p = r ^ (1 << b)
            src[r] = np.where(won[p] & ~won[r], C * p + np.arange(C), src[r])
            if r < p:
                u = np.flatnonzero(won[r] & won[p])
                low.append(C * r + u)
                high.append(C * p + u)
        low, high = np.concatenate(low), np.concatenate(high)
        if len(low):
            v = np.float32(0.5) * numbers(k, low) + np.float32(0.5) * numbers(k, high)
            k = anew(k, np.concatenate([low, high]), np.concatenate([v, v], axis=1))
        k = pick(k, src.reshape(-1))
    oc, osc, y = np.zeros((N, 128, 4 * C), np.uint8), np.zeros((N, 16, C), np.uint8), np.zeros((N, 128, O * C), np.float32)
    for r in range(N):
        t = pick(k, C * r + np.arange(C))
        oc[r], osc[r] = emit(t)
        for o in range(O): y[r, :, C * o:C * o + C] = mx_ref.matmul(mx_ref.quantize(np.ascontiguousarray(cut(w[r], o))), t)
    return {"oc": oc, "osc": osc, "ch": ch, "y": y}

@@ -1,0 +1,407 @@
+from concourse.bass import DstId, RemoteDMATransfer
+from concourse.mybir import dt, AluOpType, ActivationFunctionType
+
+R = 3
+F8, U8, U16, BF, F32, I32 = "float8_e4m3fn_x4", "uint8", "uint16", "bfloat16", "float32", "int32"
+
+SCRATCH = {
+    "kbs": ("sbuf", [128, 512], BF), "xs": ("sbuf", [128, 512], BF), "ws": ("sbuf", [128, 512], BF),
+    "zh": ("sbuf", [128, 128], BF), "zf": ("sbuf", [128, 516], BF),
+    "hbc": ("sbuf", [128, 512], F8), "hbs": ("sbuf", [128, 512], U8),
+    "iq": ("sbuf", [128, 48], I32), "kk": ("sbuf", [128, 48], I32), "k8": ("sbuf", [128, 8], I32),
+    "q15": ("sbuf", [128, 48], I32), "q31": ("sbuf", [128, 4], I32), "lxi": ("sbuf", [128, 48], I32),
+    "lx": ("sbuf", [128, 48], U16), "c8": ("sbuf", [128, 8], F32), "cf": ("sbuf", [128, 8], F32),
+    "lo": ("sbuf", [128, 4], F32), "hi": ("sbuf", [128, 4], F32), "wt": ("sbuf", [128, 4], F32),
+    "uc": ("sbuf", [128, 256], BF), "dr": ("sbuf", [128, 256], BF), "du": ("sbuf", [128, 256], BF),
+    "xqc": ("sbuf", [128, 128], F8), "xqs": ("sbuf", [128, 128], U8),
+    "wqc": ("sbuf", [128, 128], F8), "wqs": ("sbuf", [128, 128], U8),
+    "dtk": ("sbuf", [128, 384], BF),
+    "fc": ("sbuf", [128, 128], F8), "fs": ("sbuf", [128, 128], U8), "ys": ("sbuf", [128, 128], F32),
+    "zc": ("sbuf", [128, 128], F8), "zs": ("sbuf", [128, 128], U8),
+    "scn": ("sbuf", [128, 768], F32), "jnk": ("sbuf", [128, 768], BF), "cnt": ("sbuf", [128, 12], F32),
+    "nt": ("sbuf", [128, 512], BF), "mt": ("sbuf", [128, 512], BF),
+    "ps0": ("psum", [128, 512], F32), "ps1": ("psum", [128, 512], F32), "py": ("psum", [128, 512], F32), "pe": ("psum", [128, 512], F32),
+    "pd0": ("psum", [128, 512], F32), "pd1": ("psum", [128, 512], F32), "pd2": ("psum", [128, 512], F32), "pd3": ("psum", [128, 512], F32),
+}
+for _b in range(R):
+    SCRATCH.update({
+        "xrc%d" % _b: ("sbuf", [128, 256], F8), "xrs%d" % _b: ("sbuf", [128, 256], U8),
+        "kwc%d" % _b: ("sbuf", [128, 256], F8), "kws%d" % _b: ("sbuf", [128, 256], U8),
+        "wc%d" % _b: ("sbuf", [128, 288], F8), "wsc%d" % _b: ("sbuf", [128, 288], U8),
+        "d75_%d" % _b: ("sbuf", [128, 512], BF),
+        "of%d" % _b: ("sbuf", [128, 2], U16), "pl%d" % _b: ("sbuf", [128, 2], U16),
+        "la%d" % _b: ("sbuf", [128, 8], U16), "lf%d" % _b: ("sbuf", [128, 8], U16),
+        "hl%d" % _b: ("sbuf", [128, 2], U16), "hc%d" % _b: ("sbuf", [128, 32], F8), "hz%d" % _b: ("sbuf", [128, 128], U8),
+    })
+    for _s in "op":
+        SCRATCH.update({"%sv%d" % (_s, _b): ("sbuf", [128, 4], F32), "%sa%d" % (_s, _b): ("sbuf", [128, 256], BF),
+                        "%st%d" % (_s, _b): ("sbuf", [128, 256], BF), "%sm%d" % (_s, _b): ("sbuf", [128, 256], BF),
+                        "%sw%d" % (_s, _b): ("sbuf", [128, 24], F32)})
+
+SEMAPHORES = ["ms", "zr", "zm", "xt", "zn", "lx", "wl", "ldk", "ldx", "ldw", "io", "zfd", "cs", "c8", "hb0", "hb1", "hb2", "hb3", "qk", "qx", "qw",
+              "d0", "d1", "d2", "d3", "e0", "e1", "e2", "e3", "t0", "t1", "t2", "t3", "f0", "f1", "f2", "f3", "s0", "s1",
+              "m0", "m1", "m2", "m3", "n0", "n1", "n2", "n3", "sc0", "sc1", "ac0", "ac1", "cv", "ov", "ga", "qn", "vl", "vp",
+              "oc", "pa", "pz", "zq", "pc", "ps", "zd", "qm", "pf", "pg", "ym", "ye", "st", "loc", "ucd", "iq"]
+for _b in range(R):
+    SEMAPHORES += ["%s%d" % (_n, _b) for _n in ("hl", "hc", "hz", "rl", "rc", "rz", "xca", "xcb", "xza", "xzb")]
+
+
+def helpers(core, dst, T, topo):
+    c = [h for h in topo.cores_of(core) if T.rank_of(h) is None and topo.die(h) == topo.die(core) and topo.may_write(h, dst)]
+    return c[0], c[-1]
+
+
+def bits(engines):
+    return sum(1 << e for e in engines)
+
+
+def parts(engines):
+    n = len(engines) // 2
+    return engines[:n], engines[n:]
+
+
+def hand_on(g, core, T, topo):
+    home = [c for c in topo.cores_of(core) if T.rank_of(c) is not None]
+    if not home:
+        return
+    r, sent = T.rank_of(home[0]), 0
+    for b in range(R):
+        dst = T.cores[r ^ (1 << b)]
+        ha, hb = helpers(home[0], dst, T, topo)
+        if core not in (ha, hb):
+            continue
+        rid, pid = topo.addr(dst, core)
+        eng = topo.engines(core, dst)
+        inn = topo.engines(home[0], core)
+        pc, pz = parts(inn)
+        cols = slice(0, 2) if b else (slice(0, 1) if core == ha else slice(1, 2))
+        if b == 0 or core == hb:
+            g.wait_ge(T.sem["hl%d" % b], len(inn) if b else len(inn) // 2)
+            g.remote_dma(T["pl%d" % b][:, cols], T["hl%d" % b][:, cols], T.sem["rl%d" % b], T.sem["loc"], pid, rid, bits(eng))
+            sent += len(eng)
+        if core == ha:
+            g.wait_ge(T.sem["hc%d" % b], len(pc))
+            g.remote_dma(T["wc%d" % b][:, 128:160].bitcast(dt.uint8), T["hc%d" % b][:, 0:32].bitcast(dt.uint8),
+                         T.sem["rc%d" % b], T.sem["loc"], pid, rid, bits(eng))
+        else:
+            g.wait_ge(T.sem["hz%d" % b], len(pz))
+            g.remote_dma(T["wsc%d" % b][:, 128:160], T["hz%d" % b][:, 96:128],
+                         T.sem["rz%d" % b], T.sem["loc"], pid, rid, bits(eng))
+        sent += len(eng)
+    if sent:
+        g.wait_ge(T.sem["loc"], sent)
+
+
+def rank_program(g, core, T, topo):
+    rank = T.rank_of(core)
+    if rank is None:
+        hand_on(g, core, T, topo)
+        return
+    A, F = AluOpType, ActivationFunctionType
+    V, S, E, Y = g.vector, g.scalar, g.tensor, g.sync
+    cnt, seen, qn = {}, {}, {"V": V, "S": S, "E": E, "Y": Y, "g": g}
+
+    def up(ins, name, n=1):
+        ins.then_inc(T.sem[name], n)
+        cnt[name] = cnt.get(name, 0) + n
+
+    def wt(q, *names):
+        for m in names:
+            if cnt.get(m, 0) > seen.get((q, m), 0):
+                qn[q].wait_ge(T.sem[m], cnt[m])
+                seen[(q, m)] = cnt[m]
+
+    def due(name, n):
+        cnt[name] = cnt.get(name, 0) + n
+
+    def mx(out, lc, ls, rc, rs, name, start=True, stop=True):
+        up(E.matmul_mx(out, lc, ls, rc, rs, start, stop), name)
+
+    def hb(b):
+        return T.hbc[:, 128 * b:128 * b + 128], T.hbs[:, 128 * b:128 * b + 128]
+
+    def make_hb(b):
+        wt("V", "zfd")
+        up(V.quantize_mx(*hb(b), T.zf[:, 3 - b:515 - b]), "hb%d" % b)
+
+    def send(h, e, sem, src, dst):
+        rid, pid = topo.addr(h, core)
+        due("loc", len(e))
+        return RemoteDMATransfer(dst_ids=[DstId(rid=rid, pnc=pid)], dma_engine_mask=bits(e), remote_sem=T.sem[sem], src=src, dst=dst)
+
+    pd = [T["pd%d" % b] for b in range(4)]
+    px = [T.py, T.pe, T.ps0, T.ps1]
+
+    up(S.dma_start(T.xs[:, 0:384], T.x[:]), "ldx", 16)
+    up(Y.dma_start(T.kbs[:], T.kb[:]), "ldk", 16)
+    up(Y.dma_start(T.ws[:], T.w[:]), "ldw", 16)
+    up(g.iota(T.iq[:], [[0, 48]], 0, 1), "iq")
+    up(g.iota(T.kk[:], [[32, 3], [16, 2], [0, 8]], 0, 0), "iq")
+    up(V.memset(T.zf[:], 0.0), "ms")
+    up(V.memset(T.zh[:], 0.5), "ms")
+    wt("g", "ms")
+    up(g.affine_select(T.zf[:, 3:515:4], T.zh[:], [[-1, 128]], A.is_equal, 0.0, 0, 1), "zfd")
+    up(g.iota(T.uc[:], [[16, 8], [0, 2], [1, 16]], 0, 0, allow_small_or_imprecise_dtypes=True), "ucd")
+    up(g.iota(T.k8[:], [[16, 8]], 0, 0), "io")
+    up(V.memset(T.xs[:, 384:512], 0.0), "xt")
+    wt("V", "iq")
+    up(V.tensor_scalar(T.q15[:], T.iq[:], 15, None, A.bitwise_and), "cs")
+    up(V.tensor_scalar(T.q31[:, 0:1], T.iq[:, 0:1], 31, None, A.bitwise_and), "cs")
+    up(V.memset(T.nt[:, 0:128], 0.0), "zn")
+    wt("V", "cs")
+    up(V.tensor_tensor(T.lxi[:], T.q15[:], T.kk[:], A.add), "cs")
+    make_hb(0)
+    wt("V", "cs")
+    up(V.tensor_copy(T.lx[:], T.lxi[:]), "lx")
+    make_hb(1)
+
+    def pick_c(b, h):
+        wt("V", "qx", "lx")
+        up(V.tensor_copy(T["xrc%d" % b][:, 128 * h:128 * h + 128].bitcast(dt.uint32),
+                         T.xqc[:].bitcast(dt.uint32).indirect(T.lx[:, 16 * b + 8 * h:16 * b + 8 * h + 8])), "xc%s%d" % ("ab"[h], b))
+
+    def pick_z(b, h):
+        wt("S", "qx", "lx")
+        up(S.activation(T["xrs%d" % b][:, 128 * h:128 * h + 128],
+                        T.xqs[:].indirect(T.lx[:, 16 * b + 8 * h:16 * b + 8 * h + 8]), F.Copy), "xz%s%d" % ("ab"[h], b))
+
+    wt("V", "ldx", "xt")
+    up(V.quantize_mx(T.xqc[:], T.xqs[:], T.xs[:]), "qx")
+    wt("V", "ldk")
+    up(V.quantize_mx(T.kwc0[:, 128:256], T.kws0[:, 128:256], T.kbs[:]), "qk")
+    pick_c(0, 0)
+    pick_c(0, 1)
+    pick_z(0, 0)
+    pick_z(0, 1)
+    make_hb(2)
+    make_hb(3)
+
+    def ev_v(out, src, d, e, scale):
+        wt("V", d)
+        up(V.tensor_scalar(out, src, scale, None, A.mult), e)
+
+    def ev_s(out, src, d, e, scale):
+        wt("S", d)
+        up(S.activation(out, src, F.Copy, scale=scale), e)
+
+    def stepper(chain):
+        def step(f, *names):
+            def go():
+                wt("V", chain, *names)
+                up(f(), chain)
+            return go
+        return step
+
+    def slots(o, b, step, data, op, *names):
+        v, a, t, m = (T["%s%s%d" % (o, n, b)] for n in "vatm")
+        return [step(lambda: V.tensor_scalar(a[:], T.uc[:], v[:, 1:2], T.wt[:, 0:1], A.is_equal, A.mult), "ucd", *names),
+                step(lambda: V.transpose(t[:], a[:])),
+                step(lambda: V.tensor_tensor_scan(m[:], data[:], t[:], -1000.0, op, A.min), "zr", "c8")], m[:, 31:256:32]
+
+    for b in range(R):
+        KC, KS, WC, WS = (T["%s%d" % (n, b)] for n in ("kwc", "kws", "wc", "wsc"))
+        XC, XS, D75 = (T["%s%d" % (n, b)] for n in ("xrc", "xrs", "d75_"))
+        OF, PL, LA, LF, ov, pv = (T["%s%d" % (n, b)] for n in ("of", "pl", "la", "lf", "ov", "pv"))
+        NT, MT = T.nt, T.mt
+        dst = T.cores[rank ^ (1 << b)]
+        h0, h1 = helpers(core, dst, T, topo)
+        G = (KC[:, 128:256], KS[:, 128:256])
+
+        def dG(k):
+            wt("E", "e%d" % k, "hb%d" % k)
+            mx(pd[k][:, 0:128], *hb(k), *G, "d%d" % k)
+
+        def score(h):
+            wt("E", "sc%d" % h, "n%d" % (2 + h), "xc%s%d" % ("ab"[h], b), "xz%s%d" % ("ab"[h], b))
+            mx(T["ps%d" % h][:, 0:128], XC[:, 128 * h:128 * h + 128], XS[:, 128 * h:128 * h + 128], *G, "s%d" % h)
+
+        def d75(k):
+            return D75[:, 128 * k:128 * k + 128], pd[k][:, 0:128], "d%d" % k, "e%d" % k, 1.5
+
+        def sign(h):
+            j = 2 * b + h
+            wt("S", "sc%d" % h)
+            up(S.activation(T.jnk[:, 128 * j:128 * j + 128], T.scn[:, 128 * j:128 * j + 128], F.Sign,
+                            bias=T.scn[:, 128 * j + 127:128 * j + 128], scale=-1.0, accum_out=T.cnt[:, 4 * b + h:4 * b + h + 1]), "ac%d" % h)
+
+        def scan(h):
+            j = 2 * b + h
+            wt("V", "s%d" % h, "zn")
+            up(V.tensor_tensor_scan(T.scn[:, 128 * j:128 * j + 128], T["ps%d" % h][:, 0:128], T.nt[:, 0:128], -1e29, A.max, A.add), "sc%d" % h)
+
+        def new(k):
+            wt("V", "cv", "e%d" % k, "f%d" % k)
+            up(V.tensor_tensor(NT[:, 384 + k:512:4], D75[:, 128 * k:128 * k + 128].indirect(OF[:, 0:2]),
+                               T.dtk[:, 96 * k + 32 * b:96 * k + 32 * b + 32], A.add), "ga")
+
+        if b == 0:
+            pt = [pd[2], pd[3], T.py, T.pe]
+
+            def dT(k):
+                wt("E", "qx", "hb%d" % k)
+                mx(pt[k][:, 0:128], *hb(k), T.xqc[:], T.xqs[:], "t%d" % k)
+
+            evt = [(T.dtk[:, 96 * k:96 * k + 96], pt[k][:, 0:96], "t%d" % k, "f%d" % k, 0.5) for k in range(4)]
+            dT(0)
+            dT(1)
+            wt("E", "qk")
+            score(0)
+            score(1)
+            dG(0)
+            dG(1)
+            dT(2)
+            dT(3)
+            ev_s(*evt[0])
+            ev_s(*evt[1])
+            wt("E", "f0", "f1")
+            dG(2)
+            dG(3)
+            scan(0)
+            scan(1)
+            sign(0)
+            sign(1)
+            up(V.tensor_scalar(T.lo[:, 0:1], T.q31[:, 0:1], 16, None, A.is_lt), "wl")
+            up(V.tensor_scalar(T.hi[:, 0:1], T.q31[:, 0:1], 16, None, A.is_ge), "wl")
+            up(V.tensor_scalar(T.wt[:, 0:1], T.q31[:, 0:1], -256, None, A.add), "wl")
+            ev_v(*d75(0))
+        else:
+            wt("E", "pf", "pg")
+            score(0)
+            score(1)
+            for k in range(4):
+                dG(k)
+            if b == 1:
+                pick_c(2, 1)
+            else:
+                wt("V", "ldw")
+                up(V.quantize_mx(T.wqc[:], T.wqs[:], T.ws[:]), "qw")
+            scan(0)
+            scan(1)
+            sign(0)
+            sign(1)
+            ev_v(*d75(0))
+            ev_v(*d75(2))
+        wt("S", "ac0", "wl")
+        up(S.activation(ov[:, 0:1], T.cnt[:, 4 * b:4 * b + 1], F.Copy, scale=T.lo[:, 0:1]), "ov")
+        ev_s(*d75(1))
+        ev_s(*d75(3))
+        wt("S", "ac1", "ov")
+        up(S.activation(ov[:, 1:2], T.cnt[:, 4 * b + 1:4 * b + 2], F.Identity, bias=ov[:, 0:1], scale=T.hi[:, 0:1]), "ov")
+        if b == 0:
+            ev_s(*evt[3])
+        wt("V", "ac0", "ac1")
+        up(V.tensor_copy(OF[:, 0:2], T.cnt[:, 4 * b:4 * b + 2]), "cv")
+        wt("g", "cv")
+        if b == 0:
+            tr = []
+            for j, h in enumerate((h0, h1)):
+                e = topo.engines(core, h)
+                n = len(e) // 2
+                tr.append(send(h, e[j * n:j * n + n], "hl%d" % b, OF[:, j:j + 1], T["hl%d" % b][:, j:j + 1]))
+            g.remote_dma_fused(tr, local_sem=T.sem["loc"])
+        else:
+            rid, pid = topo.addr(h1, core)
+            e = topo.engines(core, h1)
+            g.remote_dma(T["hl%d" % b][:, 0:2], OF[:, 0:2], T.sem["hl%d" % b], T.sem["loc"], pid, rid, bits(e))
+            due("loc", len(e))
+
+        if b == 0:
+            up(V.memset(T.nt[:, 128:384], 0.0), "zn")
+            ev_v(*d75(2))
+            ev_v(*evt[2])
+        w = T["ow%d" % b]
+        step = stepper("vl")
+        steps, m = slots("o", b, step, T.du, A.max, "ov", "wl")
+        for k in (0, 2, 1, 3):
+            new(k)
+        steps[0]()
+        wt("V", "ga", "zn")
+        up(V.quantize_mx(KC[:, 0:128], KS[:, 0:128], NT[:]), "qn")
+        wt("g", "qn")
+        ec, ez = parts(topo.engines(core, h0))
+        g.remote_dma_fused([
+            send(h0, ec, "hc%d" % b, KC[:, 96:128].bitcast(dt.uint8), T["hc%d" % b][:, 0:32].bitcast(dt.uint8)),
+            send(h1, ez, "hz%d" % b, KS[:, 0:128], T["hz%d" % b][:, 0:128])], local_sem=T.sem["loc"])
+        for h in range(2):
+            wt("Y", "ac%d" % h)
+            up(Y.dma_start(T.ch[b:b + 1, 16 * h:16 * h + 16], T.cnt[0:16, 4 * b + h:4 * b + h + 1]), "st", 16)
+
+        steps[1]()
+        if b == 0:
+            wt("V", "io")
+            up(V.tensor_tensor(T.c8[:], T.q15[:, 0:8], T.k8[:], A.add), "c8")
+            up(V.memset(T.du[:], -1000.0), "zr")
+            wt("V", "c8", "zr")
+            up(V.tensor_scalar(T.du[:, 0:256:32], T.c8[:], -224.0, None, A.add), "c8")
+            up(V.memset(T.dr[:], 1.0), "zr")
+        steps[2]()
+        step(lambda: V.tensor_scalar(LA[:], m, 256.0, None, A.add))()
+        up(V.tensor_scalar(w[:, 8:16], m, -224.0, 32.0, A.is_ge, A.mult), "oc")
+        wt("V", "vl", "qn")
+        wt("S", "vl", "qn")
+        up(V.tensor_copy(WC[:, 160:288].bitcast(dt.uint32), KC[:, 96:256].bitcast(dt.uint32).indirect(LA[:])), "pa")
+        up(S.activation(WS[:, 160:288], KS[:, 96:256].indirect(LA[:]), F.Copy), "pz")
+        if b == 0:
+            up(V.memset(MT[:], 0.0), "zm")
+            pick_c(1, 0)
+            wt("V", "zm")
+            up(V.quantize_mx(T.zc[:], T.zs[:], MT[:]), "zq")
+            up(V.memset(T.dr[:, 0:256:32], 0.0), "zr")
+            up(V.tensor_scalar(T.cf[:], T.c8[:], -192.0, None, A.add), "c8")
+            pick_c(1, 1)
+            pick_c(2, 0)
+            for k in range(2):
+                for h in range(2):
+                    pick_z(1 + k, h)
+
+        no = len(topo.engines(helpers(dst, core, T, topo)[0], core))
+        due("rl%d" % b, no if b else 2 * no)
+        wt("V", "rl%d" % b, "pa", "zq", "zd")
+        wt("S", "rl%d" % b, "pz", "zq", "zd")
+        up(V.tensor_copy(T.zc[:, 0:32].bitcast(dt.uint32), WC[:, 160:288].bitcast(dt.uint32).indirect(PL[:, 0:2])), "pc")
+        up(S.activation(T.zs[:, 0:32], WS[:, 160:288].indirect(PL[:, 0:2]), F.Copy), "ps")
+        wt("E", "pc", "ps", "sc0", "sc1", "f0", "f1", "f2", "f3", "n0", "n1", "n2", "n3")
+        for k in range(4):
+            mx(px[k][:, 0:128], *hb(k), T.zc[:], T.zs[:], "zd", True, False)
+        u = T["pw%d" % b]
+        step = stepper("vp")
+        step(lambda: V.tensor_scalar(pv[:, 0:1], PL[:, 0:1], T.lo[:, 0:1], None, A.mult))()
+        step(lambda: V.tensor_scalar(pv[:, 1:2], PL[:, 1:2], T.hi[:, 0:1], pv[:, 0:1], A.mult, A.add))()
+        steps, m = slots("p", b, step, T.dr, A.mult)
+        for go in steps:
+            go()
+        step(lambda: V.tensor_tensor(u[:, 0:8], m, w[:, 8:16], A.add), "oc")()
+        step(lambda: V.tensor_tensor(u[:, 8:16], u[:, 0:8], T.cf[:], A.min), "c8")()
+
+        due("rc%d" % b, no)
+        due("rz%d" % b, no)
+        wt("E", "rc%d" % b, "rz%d" % b)
+        wt("S", "zm", "qm")
+        for k in range(4):
+            mx(px[k][:, 0:128], *hb(k), WC[:, 128:256], WS[:, 128:256], "m%d" % k, False, True)
+            wt("S", "m%d" % k)
+            up(S.activation(MT[:, 384 + k:512:4], px[k][:, 0:32], F.Copy), "n%d" % k)
+        wt("V", "n0", "n1", "n2", "n3")
+        up(V.quantize_mx(WC[:, 0:128], WS[:, 0:128], MT[:]), "qm")
+        step(lambda: V.tensor_scalar(LF[:], u[:, 8:16], 256.0, None, A.add))()
+        wt("V", "qm", "vp")
+        wt("S", "qm", "vp")
+        oc, os = (T["kwc%d" % (b + 1)][:, 128:256], T["kws%d" % (b + 1)][:, 128:256]) if b + 1 < R else (T.fc[:], T.fs[:])
+        up(V.tensor_copy(oc.bitcast(dt.uint32), WC[:, 96:288].bitcast(dt.uint32).indirect(LF[:])), "pf")
+        up(S.activation(os, WS[:, 96:288].indirect(LF[:]), F.Copy), "pg")
+
+    wt("E", "pf", "pg", "qw", "n0")
+    mx(T.py[:, 0:128], T.wqc[:], T.wqs[:], T.fc[:], T.fs[:], "ym")
+    wt("Y", "pf")
+    up(Y.dma_start(T.oc[:], T.fc[:].bitcast(dt.uint8)), "st", 16)
+    wt("S", "pg")
+    for k in range(4):
+        up(S.dma_start(T.osc[4 * k:4 * k + 4, :], T.fs[32 * k:32 * k + 4, :]), "st", 16)
+    wt("V", "ym")
+    up(V.tensor_copy(T.ys[:], T.py[:, 0:128]), "ye")
+    wt("Y", "ye")
+    up(Y.dma_start(T.y[:], T.ys[:]), "st", 16)
+    wt("Y", "st")
+    for m in sorted(cnt):
+        if max([seen.get((q, m), 0) for q in qn]) < cnt[m]:
+            wt("g", m)

@@ -4,44 +4,36 @@ from concourse.mybir import dt, AluOpType, ActivationFunctionType
 R = 3
 F8, U8, U16, BF, F32, I32 = "float8_e4m3fn_x4", "uint8", "uint16", "bfloat16", "float32", "int32"
 
-SCRATCH = {
-    "kbs": ("sbuf", [128, 512], BF), "xs": ("sbuf", [128, 512], BF), "ws": ("sbuf", [128, 512], BF),
-    "zh": ("sbuf", [128, 128], BF), "zf": ("sbuf", [128, 516], BF),
-    "hbc": ("sbuf", [128, 512], F8), "hbs": ("sbuf", [128, 512], U8),
-    "iq": ("sbuf", [128, 48], I32), "kk": ("sbuf", [128, 48], I32), "k8": ("sbuf", [128, 8], I32),
-    "q15": ("sbuf", [128, 48], I32), "q31": ("sbuf", [128, 4], I32), "lxi": ("sbuf", [128, 48], I32),
-    "lx": ("sbuf", [128, 48], U16), "c8": ("sbuf", [128, 8], F32), "cf": ("sbuf", [128, 8], F32),
-    "lo": ("sbuf", [128, 4], F32), "hi": ("sbuf", [128, 4], F32), "wt": ("sbuf", [128, 4], F32),
-    "uc": ("sbuf", [128, 256], BF), "dr": ("sbuf", [128, 256], BF), "du": ("sbuf", [128, 256], BF),
-    "xqc": ("sbuf", [128, 128], F8), "xqs": ("sbuf", [128, 128], U8),
-    "wqc": ("sbuf", [128, 128], F8), "wqs": ("sbuf", [128, 128], U8),
-    "dtk": ("sbuf", [128, 384], BF),
-    "fc": ("sbuf", [128, 128], F8), "fs": ("sbuf", [128, 128], U8), "ys": ("sbuf", [128, 128], F32),
-    "zc": ("sbuf", [128, 128], F8), "zs": ("sbuf", [128, 128], U8),
-    "scn": ("sbuf", [128, 768], F32), "jnk": ("sbuf", [128, 768], BF), "cnt": ("sbuf", [128, 12], F32),
-    "nt": ("sbuf", [128, 512], BF), "mt": ("sbuf", [128, 512], BF),
-    "ps0": ("psum", [128, 512], F32), "ps1": ("psum", [128, 512], F32), "py": ("psum", [128, 512], F32), "pe": ("psum", [128, 512], F32),
-    "pd0": ("psum", [128, 512], F32), "pd1": ("psum", [128, 512], F32), "pd2": ("psum", [128, 512], F32), "pd3": ("psum", [128, 512], F32),
-}
-for _b in range(R):
-    SCRATCH.update({
-        "xrc%d" % _b: ("sbuf", [128, 256], F8), "xrs%d" % _b: ("sbuf", [128, 256], U8),
-        "kwc%d" % _b: ("sbuf", [128, 256], F8), "kws%d" % _b: ("sbuf", [128, 256], U8),
-        "wc%d" % _b: ("sbuf", [128, 288], F8), "wsc%d" % _b: ("sbuf", [128, 288], U8),
-        "d75_%d" % _b: ("sbuf", [128, 512], BF),
-        "of%d" % _b: ("sbuf", [128, 2], U16), "pl%d" % _b: ("sbuf", [128, 2], U16),
-        "la%d" % _b: ("sbuf", [128, 8], U16), "lf%d" % _b: ("sbuf", [128, 8], U16),
-        "hl%d" % _b: ("sbuf", [128, 2], U16), "hc%d" % _b: ("sbuf", [128, 32], F8), "hz%d" % _b: ("sbuf", [128, 128], U8),
-    })
-    for _s in "op":
-        SCRATCH.update({"%sv%d" % (_s, _b): ("sbuf", [128, 4], F32), "%sa%d" % (_s, _b): ("sbuf", [128, 256], BF),
-                        "%st%d" % (_s, _b): ("sbuf", [128, 256], BF), "%sm%d" % (_s, _b): ("sbuf", [128, 256], BF),
-                        "%sw%d" % (_s, _b): ("sbuf", [128, 24], F32)})
 
-SEMAPHORES = ["ms", "zr", "zm", "xt", "zn", "lx", "wl", "ldk", "ldx", "ldw", "io", "zfd", "cs", "c8", "hb0", "hb1", "hb2", "hb3", "qk", "qx", "qw",
-              "d0", "d1", "d2", "d3", "e0", "e1", "e2", "e3", "t0", "t1", "t2", "t3", "f0", "f1", "f2", "f3", "s0", "s1",
-              "m0", "m1", "m2", "m3", "n0", "n1", "n2", "n3", "sc0", "sc1", "ac0", "ac1", "cv", "ov", "ga", "qn", "vl", "vp",
-              "oc", "pa", "pz", "zq", "pc", "ps", "zd", "qm", "pf", "pg", "ym", "ye", "st", "loc", "ucd", "iq"]
+def sb(n, d):
+    return ("sbuf", [128, n], d)
+
+
+SCRATCH = {
+    "kbs": sb(512, BF), "xs": sb(512, BF), "ws": sb(512, BF), "zh": sb(128, BF), "zf": sb(516, BF),
+    "hbc": sb(512, F8), "hbs": sb(512, U8), "iq": sb(8, I32), "k8": sb(8, I32), "q15": sb(8, I32), "q31": sb(4, I32),
+    "lx": sb(48, U16), "cf": sb(8, F32), "lo": sb(4, F32), "hi": sb(4, F32), "wt": sb(4, F32),
+    "hf": sb(2, F32), "pf": sb(2, F32), "mk": sb(4, F32), "tb": sb(256, BF),
+    "uc": sb(256, BF), "dp": sb(256, BF), "du": sb(256, BF),
+    "xqc": sb(128, F8), "xqs": sb(128, U8), "wqc": sb(128, F8), "wqs": sb(128, U8), "dtk": sb(384, BF),
+    "fc": sb(128, F8), "fs": sb(128, U8), "ys": sb(128, F32), "zc": sb(128, F8), "zs": sb(128, U8),
+    "scn": sb(768, F32), "jnk": sb(768, BF), "cnt": sb(12, F32), "nt": sb(512, BF), "mt": sb(512, BF),
+}
+for _n in ("ps0", "ps1", "py", "pe", "pd0", "pd1", "pd2", "pd3"):
+    SCRATCH[_n] = ("psum", [128, 512], F32)
+for _b in range(R):
+    for _n, _w, _d in (("xrc", 256, F8), ("xrs", 256, U8), ("kwc", 256, F8), ("kws", 256, U8), ("wc", 288, F8), ("wsc", 288, U8),
+                       ("d75_", 512, BF), ("of", 2, U16), ("pl", 2, U16), ("la", 8, U16), ("lf", 8, U16),
+                       ("hl", 2, U16), ("hc", 32, F8), ("hz", 128, U8),
+                       ("ov", 4, F32), ("oa", 256, BF), ("ot", 256, BF), ("om", 256, BF), ("ow", 8, F32),
+                       ("pv", 4, F32), ("pa", 256, BF), ("pt", 256, BF), ("pm", 256, BF), ("pw", 8, F32)):
+        SCRATCH["%s%d" % (_n, _b)] = sb(_w, _d)
+
+SEMAPHORES = ["ms", "mz", "mk", "tb", "pu", "zm", "eq", "fp", "xt", "zn", "lx", "wl", "ldk", "ld0", "ldx", "ldw", "io", "zfd", "cs", "c8",
+              "qk", "q0", "qx", "qw", "s0", "s1", "sc0", "sc1", "ac0", "ac1", "cv", "ov", "ga", "qn", "vl", "vp", "v0", "v1",
+              "oc", "dp", "fl", "pa", "pz", "pc", "ps", "zd", "qm", "pf", "pg", "ym", "ye", "st", "loc", "ucd", "iq"]
+for _b in range(4):
+    SEMAPHORES += ["%s%d" % (_n, _b) for _n in ("hb", "d", "e", "t", "f", "m", "n")]
 for _b in range(R):
     SEMAPHORES += ["%s%d" % (_n, _b) for _n in ("hl", "hc", "hz", "rl", "rc", "rz", "xca", "xcb", "xza", "xzb")]
 
@@ -74,10 +66,9 @@ def hand_on(g, core, T, topo):
         eng = topo.engines(core, dst)
         inn = topo.engines(home[0], core)
         pc, pz = parts(inn)
-        cols = slice(0, 2) if b else (slice(0, 1) if core == ha else slice(1, 2))
-        if b == 0 or core == hb:
-            g.wait_ge(T.sem["hl%d" % b], len(inn) if b else len(inn) // 2)
-            g.remote_dma(T["pl%d" % b][:, cols], T["hl%d" % b][:, cols], T.sem["rl%d" % b], T.sem["loc"], pid, rid, bits(eng))
+        if core == (hb if b else ha):
+            g.wait_ge(T.sem["hl%d" % b], len(inn))
+            g.remote_dma(T["pl%d" % b if b else "pf"][:], T["hl%d" % b if b else "hf"][:], T.sem["rl%d" % b], T.sem["loc"], pid, rid, bits(eng))
             sent += len(eng)
         if core == ha:
             g.wait_ge(T.sem["hc%d" % b], len(pc))
@@ -121,7 +112,7 @@ def rank_program(g, core, T, topo):
         return T.hbc[:, 128 * b:128 * b + 128], T.hbs[:, 128 * b:128 * b + 128]
 
     def make_hb(b):
-        wt("V", "zfd")
+        wt("V", "zfd", "mz")
         up(V.quantize_mx(*hb(b), T.zf[:, 3 - b:515 - b]), "hb%d" % b)
 
     def send(h, e, sem, src, dst):
@@ -129,52 +120,53 @@ def rank_program(g, core, T, topo):
         due("loc", len(e))
         return RemoteDMATransfer(dst_ids=[DstId(rid=rid, pnc=pid)], dma_engine_mask=bits(e), remote_sem=T.sem[sem], src=src, dst=dst)
 
+    def fill(out, c, name):
+        up(S.activation(out, T.zh[:], F.Copy, scale=2.0 * c), name)
+
     pd = [T["pd%d" % b] for b in range(4)]
     px = [T.py, T.pe, T.ps0, T.ps1]
+    NT, MT = T.nt, T.mt
 
-    up(S.dma_start(T.xs[:, 0:384], T.x[:]), "ldx", 16)
+    up(Y.dma_start(NT[:, 384:512], T.x[:, 0:128]), "ld0", 16)
     up(Y.dma_start(T.kbs[:], T.kb[:]), "ldk", 16)
-    up(Y.dma_start(T.ws[:], T.w[:]), "ldw", 16)
-    up(g.iota(T.iq[:], [[0, 48]], 0, 1), "iq")
-    up(g.iota(T.kk[:], [[32, 3], [16, 2], [0, 8]], 0, 0), "iq")
-    up(V.memset(T.zf[:], 0.0), "ms")
+    wt("Y", "ld0")
+    up(Y.dma_start(T.xs[:, 128:384], T.x[:, 128:384]), "ldx", 16)
+    up(g.iota(T.iq[:], [[0, 8]], 0, 1), "iq")
     up(V.memset(T.zh[:], 0.5), "ms")
+    for k in range(3):
+        up(V.memset(T.zf[:, k:516:4], 0.0), "mz")
+    up(V.memset(T.zf[:, 515:516], 0.0), "mz")
     wt("g", "ms")
     up(g.affine_select(T.zf[:, 3:515:4], T.zh[:], [[-1, 128]], A.is_equal, 0.0, 0, 1), "zfd")
-    up(g.iota(T.uc[:], [[16, 8], [0, 2], [1, 16]], 0, 0, allow_small_or_imprecise_dtypes=True), "ucd")
-    up(g.iota(T.k8[:], [[16, 8]], 0, 0), "io")
-    up(V.memset(T.xs[:, 384:512], 0.0), "xt")
+    up(g.iota(T.k8[:], [[16, 2], [32, 4]], 32, 0), "io")
+    for k in range(2):
+        up(g.iota(T.uc[:, 128 * k:128 * k + 128], [[-8192, 4], [0, 2], [-256, 16]], -256 - 4096 * k, 0,
+                  allow_small_or_imprecise_dtypes=True), "ucd")
+    wt("S", "ms")
+    for k in range(3):
+        fill(NT[:, 128 * k:128 * k + 128], 0.0, "zn")
+    fill(T.xs[:, 0:128], 0.0, "xt")
+    fill(T.xs[:, 384:512], 0.0, "xt")
+    for k in range(2):
+        fill(T.du[:, 128 * k:128 * k + 128], -1024.0, "fl")
     wt("V", "iq")
     up(V.tensor_scalar(T.q15[:], T.iq[:], 15, None, A.bitwise_and), "cs")
     up(V.tensor_scalar(T.q31[:, 0:1], T.iq[:, 0:1], 31, None, A.bitwise_and), "cs")
-    up(V.memset(T.nt[:, 0:128], 0.0), "zn")
     wt("V", "cs")
-    up(V.tensor_tensor(T.lxi[:], T.q15[:], T.kk[:], A.add), "cs")
-    make_hb(0)
-    wt("V", "cs")
-    up(V.tensor_copy(T.lx[:], T.lxi[:]), "lx")
-    make_hb(1)
+    for h in range(2):
+        up(V.tensor_scalar(T.lx[:, 8 * h:8 * h + 8], T.q15[:], 96 + 16 * h, None, A.add), "lx")
+    for k in range(2):
+        make_hb(k)
 
-    def pick_c(b, h):
-        wt("V", "qx", "lx")
-        up(V.tensor_copy(T["xrc%d" % b][:, 128 * h:128 * h + 128].bitcast(dt.uint32),
-                         T.xqc[:].bitcast(dt.uint32).indirect(T.lx[:, 16 * b + 8 * h:16 * b + 8 * h + 8])), "xc%s%d" % ("ab"[h], b))
+    def pick_c(b, h, n=1):
+        wt("V", "qx" if b else "q0", "lx")
+        up(V.tensor_copy(T["xrc%d" % b][:, 128 * h:128 * (h + n)].bitcast(dt.uint32),
+                         (T.xqc if b else T.zc)[:].bitcast(dt.uint32).indirect(T.lx[:, 16 * b + 8 * h:16 * b + 8 * (h + n)])), "xc%s%d" % ("ab"[h], b))
 
-    def pick_z(b, h):
-        wt("S", "qx", "lx")
-        up(S.activation(T["xrs%d" % b][:, 128 * h:128 * h + 128],
-                        T.xqs[:].indirect(T.lx[:, 16 * b + 8 * h:16 * b + 8 * h + 8]), F.Copy), "xz%s%d" % ("ab"[h], b))
-
-    wt("V", "ldx", "xt")
-    up(V.quantize_mx(T.xqc[:], T.xqs[:], T.xs[:]), "qx")
-    wt("V", "ldk")
-    up(V.quantize_mx(T.kwc0[:, 128:256], T.kws0[:, 128:256], T.kbs[:]), "qk")
-    pick_c(0, 0)
-    pick_c(0, 1)
-    pick_z(0, 0)
-    pick_z(0, 1)
-    make_hb(2)
-    make_hb(3)
+    def pick_z(b, h, n=1):
+        wt("S", "qx" if b else "q0", "lx")
+        up(S.activation(T["xrs%d" % b][:, 128 * h:128 * (h + n)],
+                        (T.xqs if b else T.zs)[:].indirect(T.lx[:, 16 * b + 8 * h:16 * b + 8 * (h + n)]), F.Copy), "xz%s%d" % ("ab"[h], b))
 
     def ev_v(out, src, d, e, scale):
         wt("V", d)
@@ -184,35 +176,61 @@ def rank_program(g, core, T, topo):
         wt("S", d)
         up(S.activation(out, src, F.Copy, scale=scale), e)
 
+    wt("V", "ld0", "zn")
+    up(V.quantize_mx(T.zc[:], T.zs[:], NT[:]), "q0")
+    make_hb(2)
+    pick_c(0, 0)
+    pick_z(0, 0)
+    pick_z(0, 1)
+    pt = [T.py, T.pe, pd[2], T.py]
+
+    def dT(k):
+        wt("E", "q0", "hb%d" % k, "f0")
+        mx(pt[k][:, 0:128], *hb(k), T.zc[:], T.zs[:], "t%d" % k)
+
+    def eT(k):
+        ev_s(T.dtk[:, 96 * k:96 * k + 32], pt[k][:, 96:128], "t%d" % k, "f%d" % k, 0.5)
+
+    for k in range(3):
+        dT(k)
+    for k in range(3):
+        eT(k)
+    wt("V", "ldk")
+    up(V.quantize_mx(T.kwc0[:, 128:256], T.kws0[:, 128:256], T.kbs[:]), "qk")
+    pick_c(0, 1)
+    up(V.tensor_scalar(T.lo[:, 0:1], T.q31[:, 0:1], 16, -256.0, A.is_lt, A.mult), "wl")
+
     def stepper(chain):
         def step(f, *names):
-            def go():
-                wt("V", chain, *names)
-                up(f(), chain)
-            return go
+            wt("V", chain, *names)
+            up(f(), chain)
         return step
 
-    def slots(o, b, step, data, op, *names):
-        v, a, t, m = (T["%s%s%d" % (o, n, b)] for n in "vatm")
-        return [step(lambda: V.tensor_scalar(a[:], T.uc[:], v[:, 1:2], T.wt[:, 0:1], A.is_equal, A.mult), "ucd", *names),
-                step(lambda: V.transpose(t[:], a[:])),
-                step(lambda: V.tensor_tensor_scan(m[:], data[:], t[:], -1000.0, op, A.min), "zr", "c8")], m[:, 31:256:32]
+    def first(m, d, t, *chain):
+        for k in range(2):
+            c = slice(128 * k, 128 * k + 128)
+            up(V.tensor_tensor_scan(m[:, c], d[:, c], t[:, c], -1024.0, A.max, A.min), chain[k % len(chain)])
 
     for b in range(R):
         KC, KS, WC, WS = (T["%s%d" % (n, b)] for n in ("kwc", "kws", "wc", "wsc"))
         XC, XS, D75 = (T["%s%d" % (n, b)] for n in ("xrc", "xrs", "d75_"))
         OF, PL, LA, LF, ov, pv = (T["%s%d" % (n, b)] for n in ("of", "pl", "la", "lf", "ov", "pv"))
-        NT, MT = T.nt, T.mt
+        oa, ot, om, w = (T["o%s%d" % (n, b)] for n in "atmw")
+        pa, ptt, pm, u = (T["p%s%d" % (n, b)] for n in "atmw")
         dst = T.cores[rank ^ (1 << b)]
         h0, h1 = helpers(core, dst, T, topo)
         G = (KC[:, 128:256], KS[:, 128:256])
 
         def dG(k):
             wt("E", "e%d" % k, "hb%d" % k)
+            if b or k == 2:
+                wt("E", "f%d" % k)
             mx(pd[k][:, 0:128], *hb(k), *G, "d%d" % k)
 
         def score(h):
-            wt("E", "sc%d" % h, "n%d" % (2 + h), "xc%s%d" % ("ab"[h], b), "xz%s%d" % ("ab"[h], b))
+            wt("E", "sc%d" % h, "n%d" % (2 + h), "xca%d" % b, "xza%d" % b)
+            if h:
+                wt("E", "xcb%d" % b, "xzb%d" % b)
             mx(T["ps%d" % h][:, 0:128], XC[:, 128 * h:128 * h + 128], XS[:, 128 * h:128 * h + 128], *G, "s%d" % h)
 
         def d75(k):
@@ -227,94 +245,66 @@ def rank_program(g, core, T, topo):
         def scan(h):
             j = 2 * b + h
             wt("V", "s%d" % h, "zn")
-            up(V.tensor_tensor_scan(T.scn[:, 128 * j:128 * j + 128], T["ps%d" % h][:, 0:128], T.nt[:, 0:128], -1e29, A.max, A.add), "sc%d" % h)
+            up(V.tensor_tensor_scan(T.scn[:, 128 * j:128 * j + 128], T["ps%d" % h][:, 0:128], NT[:, 0:128], -1e29, A.max, A.add), "sc%d" % h)
 
         def new(k):
             wt("V", "cv", "e%d" % k, "f%d" % k)
             up(V.tensor_tensor(NT[:, 384 + k:512:4], D75[:, 128 * k:128 * k + 128].indirect(OF[:, 0:2]),
                                T.dtk[:, 96 * k + 32 * b:96 * k + 32 * b + 32], A.add), "ga")
 
+        wt("E", "qk", "pf", "pg")
+        score(0)
         if b == 0:
-            pt = [pd[2], pd[3], T.py, T.pe]
-
-            def dT(k):
-                wt("E", "qx", "hb%d" % k)
-                mx(pt[k][:, 0:128], *hb(k), T.xqc[:], T.xqs[:], "t%d" % k)
-
-            evt = [(T.dtk[:, 96 * k:96 * k + 96], pt[k][:, 0:96], "t%d" % k, "f%d" % k, 0.5) for k in range(4)]
-            dT(0)
-            dT(1)
-            wt("E", "qk")
-            score(0)
-            score(1)
             dG(0)
-            dG(1)
-            dT(2)
-            dT(3)
-            ev_s(*evt[0])
-            ev_s(*evt[1])
-            wt("E", "f0", "f1")
-            dG(2)
+        score(1)
+        for k in range(0 if b else 1, 4 if b else 3):
+            dG(k)
+        if b == 1:
+            pick_c(2, 1)
+        scan(0)
+        if b == 0:
+            make_hb(3)
             dG(3)
-            scan(0)
-            scan(1)
-            sign(0)
-            sign(1)
-            up(V.tensor_scalar(T.lo[:, 0:1], T.q31[:, 0:1], 16, None, A.is_lt), "wl")
-            up(V.tensor_scalar(T.hi[:, 0:1], T.q31[:, 0:1], 16, None, A.is_ge), "wl")
+            dT(3)
+        scan(1)
+        sign(0)
+        sign(1)
+        ev_v(*d75(0))
+        if b == 0:
+            up(V.tensor_scalar(T.hi[:, 0:1], T.q31[:, 0:1], 16, -256.0, A.is_ge, A.mult), "wl")
             up(V.tensor_scalar(T.wt[:, 0:1], T.q31[:, 0:1], -256, None, A.add), "wl")
-            ev_v(*d75(0))
+            ev_s(*d75(1))
         else:
-            wt("E", "pf", "pg")
-            score(0)
-            score(1)
-            for k in range(4):
-                dG(k)
-            if b == 1:
-                pick_c(2, 1)
-            else:
-                wt("V", "ldw")
-                up(V.quantize_mx(T.wqc[:], T.wqs[:], T.ws[:]), "qw")
-            scan(0)
-            scan(1)
-            sign(0)
-            sign(1)
-            ev_v(*d75(0))
-            ev_v(*d75(2))
-        wt("S", "ac0", "wl")
-        up(S.activation(ov[:, 0:1], T.cnt[:, 4 * b:4 * b + 1], F.Copy, scale=T.lo[:, 0:1]), "ov")
-        ev_s(*d75(1))
+            ev_v(*d75(1))
+        ev_s(*d75(2))
         ev_s(*d75(3))
+        if b == 0:
+            eT(3)
+        wt("S", "ac0", "wl")
+        up(S.activation(ov[:, 0:1], T.cnt[:, 4 * b:4 * b + 1], F.Identity, bias=T.wt[:, 0:1], scale=T.lo[:, 0:1]), "ov")
         wt("S", "ac1", "ov")
         up(S.activation(ov[:, 1:2], T.cnt[:, 4 * b + 1:4 * b + 2], F.Identity, bias=ov[:, 0:1], scale=T.hi[:, 0:1]), "ov")
+        wt("S", "ov", "ucd")
+        up(S.activation(oa[:], T.uc[:], F.Abs, bias=ov[:, 1:2], scale=-1.0), "eq")
         if b == 0:
-            ev_s(*evt[3])
+            for k in range(2):
+                fill(T.dp[:, 128 * k:128 * k + 128], -1024.0, "fp")
+            up(S.activation(T.mk[:, 2:3], T.lo[:, 0:1], F.Identity, bias=-1.0), "tb")
+            for k in range(3):
+                fill(MT[:, 128 * k:128 * k + 128], 0.0, "zm")
+            wt("S", "tb")
+            up(S.activation(T.tb[:], T.uc[:], F.Identity, bias=T.mk[:, 2:3], scale=-1.0 / 256), "tb")
         wt("V", "ac0", "ac1")
         up(V.tensor_copy(OF[:, 0:2], T.cnt[:, 4 * b:4 * b + 2]), "cv")
-        wt("g", "cv")
-        if b == 0:
-            tr = []
-            for j, h in enumerate((h0, h1)):
-                e = topo.engines(core, h)
-                n = len(e) // 2
-                tr.append(send(h, e[j * n:j * n + n], "hl%d" % b, OF[:, j:j + 1], T["hl%d" % b][:, j:j + 1]))
-            g.remote_dma_fused(tr, local_sem=T.sem["loc"])
-        else:
-            rid, pid = topo.addr(h1, core)
-            e = topo.engines(core, h1)
-            g.remote_dma(T["hl%d" % b][:, 0:2], OF[:, 0:2], T.sem["hl%d" % b], T.sem["loc"], pid, rid, bits(e))
-            due("loc", len(e))
+        wt("g", *(("cv",) if b else ("ac0", "ac1")))
+        hl = h1 if b else h0
+        rid, pid = topo.addr(hl, core)
+        e = topo.engines(core, hl)
+        g.remote_dma(T["hl%d" % b if b else "hf"][:], OF[:] if b else T.cnt[:, 0:2], T.sem["hl%d" % b], T.sem["loc"], pid, rid, bits(e))
+        due("loc", len(e))
 
-        if b == 0:
-            up(V.memset(T.nt[:, 128:384], 0.0), "zn")
-            ev_v(*d75(2))
-            ev_v(*evt[2])
-        w = T["ow%d" % b]
-        step = stepper("vl")
-        steps, m = slots("o", b, step, T.du, A.max, "ov", "wl")
-        for k in (0, 2, 1, 3):
+        for k in range(4):
             new(k)
-        steps[0]()
         wt("V", "ga", "zn")
         up(V.quantize_mx(KC[:, 0:128], KS[:, 0:128], NT[:]), "qn")
         wt("g", "qn")
@@ -322,68 +312,92 @@ def rank_program(g, core, T, topo):
         g.remote_dma_fused([
             send(h0, ec, "hc%d" % b, KC[:, 96:128].bitcast(dt.uint8), T["hc%d" % b][:, 0:32].bitcast(dt.uint8)),
             send(h1, ez, "hz%d" % b, KS[:, 0:128], T["hz%d" % b][:, 0:128])], local_sem=T.sem["loc"])
-        for h in range(2):
-            wt("Y", "ac%d" % h)
-            up(Y.dma_start(T.ch[b:b + 1, 16 * h:16 * h + 16], T.cnt[0:16, 4 * b + h:4 * b + h + 1]), "st", 16)
 
-        steps[1]()
+        step = stepper("vl")
         if b == 0:
-            wt("V", "io")
-            up(V.tensor_tensor(T.c8[:], T.q15[:, 0:8], T.k8[:], A.add), "c8")
-            up(V.memset(T.du[:], -1000.0), "zr")
-            wt("V", "c8", "zr")
-            up(V.tensor_scalar(T.du[:, 0:256:32], T.c8[:], -224.0, None, A.add), "c8")
-            up(V.memset(T.dr[:], 1.0), "zr")
-        steps[2]()
-        step(lambda: V.tensor_scalar(LA[:], m, 256.0, None, A.add))()
-        up(V.tensor_scalar(w[:, 8:16], m, -224.0, 32.0, A.is_ge, A.mult), "oc")
+            wt("V", "io", "fl")
+            up(V.tensor_tensor(T.du[:, 0:256:32], T.q15[:], T.k8[:], A.add), "c8")
+            up(V.memset(T.mk[:, 0:1], 1024.0), "mk")
+        step(lambda: V.transpose(ot[:], oa[:]), "eq")
+        if b == 0:
+            wt("V", "c8")
+            up(V.tensor_scalar(T.cf[:], T.du[:, 0:256:32], -224.0, None, A.add), "c8")
+            for k in (1, 2):
+                up(V.tensor_scalar(T.lx[:, 16 * k:16 * k + 16], T.lx[:, 0:16], 32 * k - 96, None, A.add), "lx")
+        wt("V", "vl", "c8")
+        first(om, T.du, ot, "vl")
+        if b == 0:
+            wt("V", "ldx", "xt")
+            up(V.quantize_mx(T.xqc[:], T.xqs[:], T.xs[:]), "qx")
+            up(V.tensor_scalar(T.mk[:, 1:2], T.lo[:, 0:1], 3.0, 512.0, A.mult, A.add), "mk")
+        if b == 2:
+            wt("V", "ldw")
+            up(V.quantize_mx(T.wqc[:], T.wqs[:], T.ws[:]), "qw")
+        wt("V", "vl")
+        for k in range(2):
+            up(V.tensor_copy(LA[:, k:8:2], om[:, 128 * k + 31:128 * k + 128:32]), "vl")
+        up(V.tensor_scalar(w[:], om[:, 31:256:32], 32.0, 32.0, A.is_ge, A.mult), "oc")
         wt("V", "vl", "qn")
         wt("S", "vl", "qn")
         up(V.tensor_copy(WC[:, 160:288].bitcast(dt.uint32), KC[:, 96:256].bitcast(dt.uint32).indirect(LA[:])), "pa")
         up(S.activation(WS[:, 160:288], KS[:, 96:256].indirect(LA[:]), F.Copy), "pz")
+        wt("V", "oc", "vp", "fp")
+        up(V.tensor_tensor(T.dp[:, 0:256:32], T.cf[:], w[:], A.subtract), "dp")
+        if b == 1:
+            pick_z(2, 0)
         if b == 0:
-            up(V.memset(MT[:], 0.0), "zm")
-            pick_c(1, 0)
-            wt("V", "zm")
-            up(V.quantize_mx(T.zc[:], T.zs[:], MT[:]), "zq")
-            up(V.memset(T.dr[:, 0:256:32], 0.0), "zr")
-            up(V.tensor_scalar(T.cf[:], T.c8[:], -192.0, None, A.add), "c8")
-            pick_c(1, 1)
+            for k in range(4):
+                wt("E", "qx", "e%d" % k)
+                mx(pd[k][:, 0:128], *hb(k), T.xqc[:], T.xqs[:], "t%d" % k)
+                ev_s(T.dtk[:, 96 * k + 32:96 * k + 96], pd[k][:, 32:96], "t%d" % k, "f%d" % k, 0.5)
+            pick_c(1, 0, 2)
             pick_c(2, 0)
-            for k in range(2):
-                for h in range(2):
-                    pick_z(1 + k, h)
+            pick_z(1, 0, 2)
 
         no = len(topo.engines(helpers(dst, core, T, topo)[0], core))
-        due("rl%d" % b, no if b else 2 * no)
-        wt("V", "rl%d" % b, "pa", "zq", "zd")
-        wt("S", "rl%d" % b, "pz", "zq", "zd")
+        due("rl%d" % b, no)
+        step = stepper("vp")
+        if b:
+            step(lambda: V.tensor_scalar(pv[:, 0:1], PL[:, 0:1], T.lo[:, 0:1], -256.0, A.mult, A.add), "rl%d" % b)
+        else:
+            wt("V", "rl0", "mk")
+            up(V.tensor_copy(PL[:], T.pf[:]), "pu")
+            step(lambda: V.tensor_tensor_scan(pv[:, 0:2], T.mk[:, 0:2], T.pf[:], 0.0, A.add, A.min))
+        wt("V", "pu", "pa", "zd", "t0", "t1", "t2", "t3", "xca0", "xcb0")
+        wt("S", "rl%d" % b, "pu", "pz", "zd", "xza0", "xzb0")
         up(V.tensor_copy(T.zc[:, 0:32].bitcast(dt.uint32), WC[:, 160:288].bitcast(dt.uint32).indirect(PL[:, 0:2])), "pc")
         up(S.activation(T.zs[:, 0:32], WS[:, 160:288].indirect(PL[:, 0:2]), F.Copy), "ps")
+        if b == 1:
+            pick_z(2, 1)
+        wt("Y", "rl%d" % b, "ac0", "ac1")
+        if b == 0:
+            up(Y.dma_start(T.ws[:], T.w[:]), "ldw", 16)
+        for h in range(2):
+            up(Y.dma_start(T.ch[b:b + 1, 16 * h:16 * h + 16], T.cnt[0:16, 4 * b + h:4 * b + h + 1]), "st", 16)
         wt("E", "pc", "ps", "sc0", "sc1", "f0", "f1", "f2", "f3", "n0", "n1", "n2", "n3")
         for k in range(4):
             mx(px[k][:, 0:128], *hb(k), T.zc[:], T.zs[:], "zd", True, False)
-        u = T["pw%d" % b]
-        step = stepper("vp")
-        step(lambda: V.tensor_scalar(pv[:, 0:1], PL[:, 0:1], T.lo[:, 0:1], None, A.mult))()
-        step(lambda: V.tensor_scalar(pv[:, 1:2], PL[:, 1:2], T.hi[:, 0:1], pv[:, 0:1], A.mult, A.add))()
-        steps, m = slots("p", b, step, T.dr, A.mult)
-        for go in steps:
-            go()
-        step(lambda: V.tensor_tensor(u[:, 0:8], m, w[:, 8:16], A.add), "oc")()
-        step(lambda: V.tensor_tensor(u[:, 8:16], u[:, 0:8], T.cf[:], A.min), "c8")()
+        if b:
+            step(lambda: V.tensor_scalar(pv[:, 1:2], PL[:, 1:2], T.hi[:, 0:1], pv[:, 0:1], A.mult, A.add))
+        step(lambda: V.tensor_scalar(pa[:], (T.uc if b else T.tb)[:], pv[:, 1:2], T.wt[:, 0:1], A.is_equal, A.mult), "tb")
+        step(lambda: V.transpose(ptt[:], pa[:]))
+        wt("V", "vp", "dp")
+        first(pm, T.dp, ptt, "v0", "v1")
+        for k in range(2):
+            wt("V", "v%d" % k)
+            up(V.tensor_tensor(u[:, k:8:2], pm[:, 128 * k + 31:128 * k + 128:32], w[:, 4 * k:4 * k + 4], A.add), "vp")
+        step(lambda: V.tensor_scalar(LF[:], u[:], 256.0, None, A.add))
 
         due("rc%d" % b, no)
         due("rz%d" % b, no)
         wt("E", "rc%d" % b, "rz%d" % b)
-        wt("S", "zm", "qm")
+        wt("S", "qm", "zm")
         for k in range(4):
             mx(px[k][:, 0:128], *hb(k), WC[:, 128:256], WS[:, 128:256], "m%d" % k, False, True)
             wt("S", "m%d" % k)
             up(S.activation(MT[:, 384 + k:512:4], px[k][:, 0:32], F.Copy), "n%d" % k)
         wt("V", "n0", "n1", "n2", "n3")
         up(V.quantize_mx(WC[:, 0:128], WS[:, 0:128], MT[:]), "qm")
-        step(lambda: V.tensor_scalar(LF[:], u[:, 8:16], 256.0, None, A.add))()
         wt("V", "qm", "vp")
         wt("S", "qm", "vp")
         oc, os = (T["kwc%d" % (b + 1)][:, 128:256], T["kws%d" % (b + 1)][:, 128:256]) if b + 1 < R else (T.fc[:], T.fs[:])

@@ -1,4 +1,3 @@
-from concourse.bass import DstId, RemoteDMATransfer
 from concourse.mybir import dt, AluOpType, ActivationFunctionType
 
 R = 3
@@ -11,31 +10,34 @@ def sb(n, d):
 
 SCRATCH = {
     "kbs": sb(512, BF), "xs": sb(512, BF), "ws": sb(512, BF), "zh": sb(128, BF), "zf": sb(516, BF),
-    "hbc": sb(512, F8), "hbs": sb(512, U8), "iq": sb(8, I32), "k8": sb(8, I32), "q15": sb(8, I32), "q31": sb(4, I32),
-    "lx": sb(48, U16), "cf": sb(8, F32), "lo": sb(4, F32), "hi": sb(4, F32), "wt": sb(4, F32),
-    "hf": sb(2, F32), "pf": sb(2, F32), "mk": sb(4, F32), "tb": sb(256, BF),
-    "uc": sb(256, BF), "dp": sb(256, BF), "du": sb(256, BF),
+    "hbc": sb(512, F8), "hbs": sb(512, U8), "iq": sb(8, I32), "q15": sb(12, I32), "k8": sb(8, F32), "cf": sb(8, F32),
+    "lx": sb(16, U16), "cc": sb(12, F32), "hf": sb(2, F32), "pf": sb(2, F32), "uc": sb(128, BF), "uo": sb(256, F32), "up": sb(256, BF),
     "xqc": sb(128, F8), "xqs": sb(128, U8), "wqc": sb(128, F8), "wqs": sb(128, U8), "dtk": sb(384, BF),
-    "fc": sb(128, F8), "fs": sb(128, U8), "ys": sb(128, F32), "zc": sb(128, F8), "zs": sb(128, U8),
+    "fc": sb(128, F8), "fs": sb(128, U8), "ys": sb(128, F32), "yw": sb(320, F32),
     "scn": sb(768, F32), "jnk": sb(768, BF), "cnt": sb(12, F32), "nt": sb(512, BF), "mt": sb(512, BF),
+    "da": sb(512, BF), "dz": sb(128, BF), "du": sb(256, BF), "dp": sb(256, BF),
 }
 for _n in ("ps0", "ps1", "py", "pe", "pd0", "pd1", "pd2", "pd3"):
     SCRATCH[_n] = ("psum", [128, 512], F32)
 for _b in range(R):
-    for _n, _w, _d in (("xrc", 256, F8), ("xrs", 256, U8), ("kwc", 256, F8), ("kws", 256, U8), ("wc", 288, F8), ("wsc", 288, U8),
+    for _n, _w, _d in (("xrc", 256, F8), ("xrs", 256, U8), ("kwc", 256, F8), ("kws", 256, U8), ("wc", 416, F8), ("wsc", 416, U8),
                        ("d75_", 512, BF), ("of", 2, U16), ("pl", 2, U16), ("la", 8, U16), ("lf", 8, U16),
-                       ("hl", 2, U16), ("hc", 32, F8), ("hz", 128, U8),
-                       ("ov", 4, F32), ("oa", 256, BF), ("ot", 256, BF), ("om", 256, BF), ("ow", 8, F32),
-                       ("pv", 4, F32), ("pa", 256, BF), ("pt", 256, BF), ("pm", 256, BF), ("pw", 8, F32)):
+                       ("hl", 2, U16), ("hc", 32, F8), ("hz", 32, U8), ("pv", 2, F32), ("ow", 8, F32),
+                       ("oa", 256, BF), ("ot", 256, BF), ("om", 256, BF), ("pa", 256, BF), ("pt", 256, BF), ("pm", 256, BF)):
         SCRATCH["%s%d" % (_n, _b)] = sb(_w, _d)
 
-SEMAPHORES = ["ms", "mz", "mk", "tb", "pu", "zm", "eq", "fp", "xt", "zn", "lx", "wl", "ldk", "ld0", "ldx", "ldw", "io", "zfd", "cs", "c8",
-              "qk", "q0", "qx", "qw", "s0", "s1", "sc0", "sc1", "ac0", "ac1", "cv", "ov", "ga", "qn", "vl", "vp", "v0", "v1",
-              "oc", "dp", "fl", "pa", "pz", "pc", "ps", "zd", "qm", "pf", "pg", "ym", "ye", "st", "loc", "ucd", "iq"]
+SEMAPHORES = ["ms", "mz", "tb", "pu", "zm", "fp", "xt", "zn", "lx", "wl", "ldk", "ld0", "ldx", "ldw", "io", "zfd", "cs", "c8",
+              "qk", "q0", "qx", "qw", "s0", "s1", "sc0", "sc1", "ac0", "ac1", "cv", "ga", "qn", "vl", "vp", "la", "cf", "sg", "mk", "oc",
+              "fl", "dp", "pa", "pz", "pc", "ps", "zd", "qm", "pf", "pg", "ym", "ye", "st", "loc", "ucd", "iq", "g2", "g3", "da",
+              "o0", "o1", "p0", "p1", "tp"]
 for _b in range(4):
-    SEMAPHORES += ["%s%d" % (_n, _b) for _n in ("hb", "d", "e", "t", "f", "m", "n")]
+    SEMAPHORES += ["%s%d" % (_n, _b) for _n in ("hb", "d", "e", "t", "f", "m", "n", "a", "z", "y")]
 for _b in range(R):
     SEMAPHORES += ["%s%d" % (_n, _b) for _n in ("hl", "hc", "hz", "rl", "rc", "rz", "xca", "xcb", "xza", "xzb")]
+
+FIRST = "k0 q0 h0 c0 z0 z1 k1 q1 c1 h1 h2 s0 s1 G0 G1 G2 n0 n1 h3 G3 g0 g1 v0 v1 a2 o0 a3 o1"
+LATER = "s0 s1 G0 G1 G2 G3 n0 n1 g0 g1 v0 v1 a2 o0 a3 o1"
+LANE, SLOT, SIGN, PART, END, BACK, OWN, AHEAD = 0, 1, 2, 3, 4, 6, 8, 10
 
 
 def helpers(core, dst, T, topo):
@@ -47,9 +49,9 @@ def bits(engines):
     return sum(1 << e for e in engines)
 
 
-def parts(engines):
+def lanes(engines, b):
     n = len(engines) // 2
-    return engines[:n], engines[n:]
+    return (engines, engines, engines) if b else (engines[:n], engines[:n], engines[n:])
 
 
 def hand_on(g, core, T, topo):
@@ -64,20 +66,18 @@ def hand_on(g, core, T, topo):
             continue
         rid, pid = topo.addr(dst, core)
         eng = topo.engines(core, dst)
-        inn = topo.engines(home[0], core)
-        pc, pz = parts(inn)
+        el, ez, ec = lanes(topo.engines(home[0], core), b)
         if core == (hb if b else ha):
-            g.wait_ge(T.sem["hl%d" % b], len(inn))
+            g.wait_ge(T.sem["hl%d" % b], len(el))
             g.remote_dma(T["pl%d" % b if b else "pf"][:], T["hl%d" % b if b else "hf"][:], T.sem["rl%d" % b], T.sem["loc"], pid, rid, bits(eng))
             sent += len(eng)
         if core == ha:
-            g.wait_ge(T.sem["hc%d" % b], len(pc))
-            g.remote_dma(T["wc%d" % b][:, 128:160].bitcast(dt.uint8), T["hc%d" % b][:, 0:32].bitcast(dt.uint8),
+            g.wait_ge(T.sem["hc%d" % b], len(ec))
+            g.remote_dma(T["wc%d" % b][:, 256:288].bitcast(dt.uint8), T["hc%d" % b][:].bitcast(dt.uint8),
                          T.sem["rc%d" % b], T.sem["loc"], pid, rid, bits(eng))
         else:
-            g.wait_ge(T.sem["hz%d" % b], len(pz))
-            g.remote_dma(T["wsc%d" % b][:, 128:160], T["hz%d" % b][:, 96:128],
-                         T.sem["rz%d" % b], T.sem["loc"], pid, rid, bits(eng))
+            g.wait_ge(T.sem["hz%d" % b], len(ez))
+            g.remote_dma(T["wsc%d" % b][:, 256:288], T["hz%d" % b][:], T.sem["rz%d" % b], T.sem["loc"], pid, rid, bits(eng))
         sent += len(eng)
     if sent:
         g.wait_ge(T.sem["loc"], sent)
@@ -105,6 +105,9 @@ def rank_program(g, core, T, topo):
     def due(name, n):
         cnt[name] = cnt.get(name, 0) + n
 
+    def four(n):
+        return ["%s%d" % (n, k) for k in range(4)]
+
     def mx(out, lc, ls, rc, rs, name, start=True, stop=True):
         up(E.matmul_mx(out, lc, ls, rc, rs, start, stop), name)
 
@@ -115,13 +118,19 @@ def rank_program(g, core, T, topo):
         wt("V", "zfd", "mz")
         up(V.quantize_mx(*hb(b), T.zf[:, 3 - b:515 - b]), "hb%d" % b)
 
-    def send(h, e, sem, src, dst):
+    def write(h, e, sem, src, dst):
         rid, pid = topo.addr(h, core)
         due("loc", len(e))
-        return RemoteDMATransfer(dst_ids=[DstId(rid=rid, pnc=pid)], dma_engine_mask=bits(e), remote_sem=T.sem[sem], src=src, dst=dst)
+        g.remote_dma(dst, src, T.sem[sem], T.sem["loc"], pid, rid, bits(e))
 
     def fill(out, c, name):
         up(S.activation(out, T.zh[:], F.Copy, scale=2.0 * c), name)
+
+    def col(j):
+        return T.cc[:, j:j + 1]
+
+    def const(j, i, scale, bias, name):
+        up(S.activation(col(j), col(i), F.Identity, bias=bias, scale=scale), name)
 
     pd = [T["pd%d" % b] for b in range(4)]
     px = [T.py, T.pe, T.ps0, T.ps1]
@@ -138,35 +147,32 @@ def rank_program(g, core, T, topo):
     up(V.memset(T.zf[:, 515:516], 0.0), "mz")
     wt("g", "ms")
     up(g.affine_select(T.zf[:, 3:515:4], T.zh[:], [[-1, 128]], A.is_equal, 0.0, 0, 1), "zfd")
-    up(g.iota(T.k8[:], [[16, 2], [32, 4]], 32, 0), "io")
-    for k in range(2):
-        up(g.iota(T.uc[:, 128 * k:128 * k + 128], [[-8192, 4], [0, 2], [-256, 16]], -256 - 4096 * k, 0,
-                  allow_small_or_imprecise_dtypes=True), "ucd")
+    up(g.iota(T.uc[:], [[32, 4], [0, 2], [1, 16]], 8, 0, allow_small_or_imprecise_dtypes=True), "ucd")
+    up(g.iota(T.k8[:], [[16, 8]], 32, 0, allow_small_or_imprecise_dtypes=True), "io")
+    up(g.iota(T.cf[:], [[-16, 8]], -48, 0, allow_small_or_imprecise_dtypes=True), "io")
     wt("S", "ms")
     for k in range(3):
         fill(NT[:, 128 * k:128 * k + 128], 0.0, "zn")
     fill(T.xs[:, 0:128], 0.0, "xt")
     fill(T.xs[:, 384:512], 0.0, "xt")
-    for k in range(2):
-        fill(T.du[:, 128 * k:128 * k + 128], -1024.0, "fl")
     wt("V", "iq")
-    up(V.tensor_scalar(T.q15[:], T.iq[:], 15, None, A.bitwise_and), "cs")
-    up(V.tensor_scalar(T.q31[:, 0:1], T.iq[:, 0:1], 31, None, A.bitwise_and), "cs")
+    up(V.tensor_scalar(T.q15[:, 0:8], T.iq[:], 15, None, A.bitwise_and), "cs")
+    up(V.tensor_scalar(T.q15[:, 8:9], T.iq[:, 0:1], 31, None, A.bitwise_and), "cs")
     wt("V", "cs")
+    up(V.tensor_copy(T.cc[:, LANE:SLOT + 1], T.q15[:, 7:9]), "cf")
     for h in range(2):
-        up(V.tensor_scalar(T.lx[:, 8 * h:8 * h + 8], T.q15[:], 96 + 16 * h, None, A.add), "lx")
-    for k in range(2):
-        make_hb(k)
+        up(V.tensor_scalar(T.lx[:, 8 * h:8 * h + 8], T.q15[:, 0:8], 16 * h, None, A.add), "lx")
 
-    def pick_c(b, h, n=1):
+    def pick_c(b, h):
         wt("V", "qx" if b else "q0", "lx")
-        up(V.tensor_copy(T["xrc%d" % b][:, 128 * h:128 * (h + n)].bitcast(dt.uint32),
-                         (T.xqc if b else T.zc)[:].bitcast(dt.uint32).indirect(T.lx[:, 16 * b + 8 * h:16 * b + 8 * (h + n)])), "xc%s%d" % ("ab"[h], b))
+        src = T.xqc[:, 32 * b:32 * b + 32] if b else T.kwc0[:, 96:128]
+        up(V.tensor_copy(T["xrc%d" % b][:, 128 * h:128 * h + 128].bitcast(dt.uint32),
+                         src.bitcast(dt.uint32).indirect(T.lx[:, 8 * h:8 * h + 8])), "xc%s%d" % ("ab"[h], b))
 
-    def pick_z(b, h, n=1):
+    def pick_z(b, h):
         wt("S", "qx" if b else "q0", "lx")
-        up(S.activation(T["xrs%d" % b][:, 128 * h:128 * (h + n)],
-                        (T.xqs if b else T.zs)[:].indirect(T.lx[:, 16 * b + 8 * h:16 * b + 8 * (h + n)]), F.Copy), "xz%s%d" % ("ab"[h], b))
+        src = T.xqs[:, 32 * b:32 * b + 32] if b else T.kws0[:, 96:128]
+        up(S.activation(T["xrs%d" % b][:, 128 * h:128 * h + 128], src.indirect(T.lx[:, 8 * h:8 * h + 8]), F.Copy), "xz%s%d" % ("ab"[h], b))
 
     def ev_v(out, src, d, e, scale):
         wt("V", d)
@@ -176,65 +182,71 @@ def rank_program(g, core, T, topo):
         wt("S", d)
         up(S.activation(out, src, F.Copy, scale=scale), e)
 
-    wt("V", "ld0", "zn")
-    up(V.quantize_mx(T.zc[:], T.zs[:], NT[:]), "q0")
-    make_hb(2)
-    pick_c(0, 0)
-    pick_z(0, 0)
-    pick_z(0, 1)
-    pt = [T.py, T.pe, pd[2], T.py]
+    def quantise(k):
+        wt("V", *(("ldk",) if k else ("ld0", "zn")))
+        up(V.quantize_mx(T.kwc0[:, 128 * k:128 * k + 128], T.kws0[:, 128 * k:128 * k + 128], (T.kbs if k else NT)[:]), "qk" if k else "q0")
 
-    def dT(k):
-        wt("E", "q0", "hb%d" % k, "f0")
-        mx(pt[k][:, 0:128], *hb(k), T.zc[:], T.zs[:], "t%d" % k)
-
-    def eT(k):
-        ev_s(T.dtk[:, 96 * k:96 * k + 32], pt[k][:, 96:128], "t%d" % k, "f%d" % k, 0.5)
-
-    for k in range(3):
-        dT(k)
-    for k in range(3):
-        eT(k)
-    wt("V", "ldk")
-    up(V.quantize_mx(T.kwc0[:, 128:256], T.kws0[:, 128:256], T.kbs[:]), "qk")
-    pick_c(0, 1)
-    up(V.tensor_scalar(T.lo[:, 0:1], T.q31[:, 0:1], 16, -256.0, A.is_lt, A.mult), "wl")
+    def lists(k):
+        if k == 0:
+            wt("S", "cf")
+            up(S.activation(col(SIGN), col(SLOT), F.Sign, bias=-15.5), "sg")
+            for h in range(2):
+                const(BACK + h, LANE, -1.0 / 256, -h / 16.0, "sg")
+        elif k == 1:
+            wt("S", "sg")
+            for h in range(2):
+                const(OWN + h, SIGN, 8.0, col(BACK + h), "wl")
+            wt("S", "ucd", "wl")
+            for h in range(2):
+                up(S.activation(T.uo[:, 128 * h:128 * h + 128], T.uc[:], F.Identity, bias=col(OWN + h)), "tb")
+        else:
+            const(PART, LANE, 1.0 / 256, 0.0, "fl")
+            for h in range(2):
+                fill(T.du[:, 128 * h:128 * h + 128], -4.0, "fl")
+            for h in range(2):
+                const(AHEAD + h, LANE, -1.0, 32.0 - 16 * h, "mk")
+            const(END, LANE, 1.0, -16.0, "mk")
+            wt("S", "io", "fl")
+            up(S.activation(T.du[:, 0:256:32], T.k8[:], F.Identity, bias=col(PART), scale=1.0 / 256), "c8")
+            wt("S", "mk")
+            for h in range(2):
+                const(BACK + h, SIGN, 8.0, col(AHEAD + h), "wl")
+            for h in range(2):
+                fill(T.dp[:, 128 * h:128 * h + 128], 0.0, "fp")
+            wt("S", "wl")
+            for h in range(2):
+                up(S.activation(T.up[:, 128 * h:128 * h + 128], T.uc[:], F.Identity, bias=col(BACK + h)), "tp")
 
     def stepper(chain):
         def step(f, *names):
-            wt("V", chain, *names)
+            wt("V", *names, chain)
             up(f(), chain)
         return step
-
-    def first(m, d, t, *chain):
-        for k in range(2):
-            c = slice(128 * k, 128 * k + 128)
-            up(V.tensor_tensor_scan(m[:, c], d[:, c], t[:, c], -1024.0, A.max, A.min), chain[k % len(chain)])
 
     for b in range(R):
         KC, KS, WC, WS = (T["%s%d" % (n, b)] for n in ("kwc", "kws", "wc", "wsc"))
         XC, XS, D75 = (T["%s%d" % (n, b)] for n in ("xrc", "xrs", "d75_"))
-        OF, PL, LA, LF, ov, pv = (T["%s%d" % (n, b)] for n in ("of", "pl", "la", "lf", "ov", "pv"))
-        oa, ot, om, w = (T["o%s%d" % (n, b)] for n in "atmw")
-        pa, ptt, pm, u = (T["p%s%d" % (n, b)] for n in "atmw")
+        OF, PL, LA, LF, pv, w = (T["%s%d" % (n, b)] for n in ("of", "pl", "la", "lf", "pv", "ow"))
+        oa, ot, om, pa, pt, pm = (T["%s%d" % (n, b)] for n in ("oa", "ot", "om", "pa", "pt", "pm"))
         dst = T.cores[rank ^ (1 << b)]
         h0, h1 = helpers(core, dst, T, topo)
-        G = (KC[:, 128:256], KS[:, 128:256])
+        el, ez, ec = lanes(topo.engines(core, h0), b)
+        last = b + 1 == R
 
         def dG(k):
-            wt("E", "e%d" % k, "hb%d" % k)
-            if b or k == 2:
-                wt("E", "f%d" % k)
-            mx(pd[k][:, 0:128], *hb(k), *G, "d%d" % k)
+            c = 128 if b else 96
+            wt("E", "qk", "pf", "pg", "e%d" % k, "hb%d" % k, "da")
+            mx(pd[k][:, 0:256 - c], *hb(k), KC[:, c:256], KS[:, c:256], "d%d" % k)
 
         def score(h):
-            wt("E", "sc%d" % h, "n%d" % (2 + h), "xca%d" % b, "xza%d" % b)
-            if h:
-                wt("E", "xcb%d" % b, "xzb%d" % b)
-            mx(T["ps%d" % h][:, 0:128], XC[:, 128 * h:128 * h + 128], XS[:, 128 * h:128 * h + 128], *G, "s%d" % h)
+            wt("E", "sc%d" % h, "n%d" % (2 + h), "xc%s%d" % ("ab"[h], b), "xz%s%d" % ("ab"[h], b), "qk", "pf", "pg")
+            mx(T["ps%d" % h][:, 0:128], XC[:, 128 * h:128 * h + 128], XS[:, 128 * h:128 * h + 128], KC[:, 128:256], KS[:, 128:256], "s%d" % h)
 
-        def d75(k):
-            return D75[:, 128 * k:128 * k + 128], pd[k][:, 0:128], "d%d" % k, "e%d" % k, 1.5
+        def d75(k, ev):
+            c = 0 if b else 32
+            ev(D75[:, 128 * k:128 * k + 128], pd[k][:, c:c + 128], "d%d" % k, "e%d" % k, 1.5)
+            if b == 0:
+                ev(T.dtk[:, 96 * k:96 * k + 32], pd[k][:, 0:32], "d%d" % k, "e%d" % k, 0.5)
 
         def sign(h):
             j = 2 * b + h
@@ -244,177 +256,179 @@ def rank_program(g, core, T, topo):
 
         def scan(h):
             j = 2 * b + h
-            wt("V", "s%d" % h, "zn")
+            wt("V", "zn", "s%d" % h)
             up(V.tensor_tensor_scan(T.scn[:, 128 * j:128 * j + 128], T["ps%d" % h][:, 0:128], NT[:, 0:128], -1e29, A.max, A.add), "sc%d" % h)
 
-        def new(k):
-            wt("V", "cv", "e%d" % k, "f%d" % k)
-            up(V.tensor_tensor(NT[:, 384 + k:512:4], D75[:, 128 * k:128 * k + 128].indirect(OF[:, 0:2]),
-                               T.dtk[:, 96 * k + 32 * b:96 * k + 32 * b + 32], A.add), "ga")
+        def own(h):
+            wt("S", "tb", "ac%d" % h)
+            up(S.activation(oa[:, 128 * h:128 * h + 128], T.uo[:, 128 * h:128 * h + 128], F.Abs,
+                            bias=T.cnt[:, 4 * b + h:4 * b + h + 1], scale=-1.0), "o%d" % h)
 
-        wt("E", "qk", "pf", "pg")
-        score(0)
+        def turn(t, a, h, name):
+            up(V.transpose(t[:, h:256:2], a[:, 128 * h:128 * h + 128]), name)
+
+        def y_of(k, c, lo, n, ev):
+            mx(pd[k][:, 0:128], T.wqc[:], T.wqs[:], WC[:, c:c + 128], WS[:, c:c + 128], "y%d" % k)
+            return lambda: ev(T.yw[:, c + lo - 96:c + lo - 96 + n], pd[k][:, lo:lo + n], "y%d" % k, "ym", 1.0)
+
+        act = {"h": make_hb, "q": quantise, "c": lambda k: pick_c(0, k), "z": lambda k: pick_z(0, k), "k": lists,
+               "s": score, "G": dG, "n": scan, "g": sign, "v": lambda k: d75(k, ev_v), "a": lambda k: d75(k, ev_s), "o": own}
+        for a in (LATER if b else FIRST).split():
+            act[a[0]](int(a[1]))
         if b == 0:
-            dG(0)
-        score(1)
-        for k in range(0 if b else 1, 4 if b else 3):
-            dG(k)
+            lists(2)
         if b == 1:
-            pick_c(2, 1)
-        scan(0)
-        if b == 0:
-            make_hb(3)
-            dG(3)
-            dT(3)
-        scan(1)
-        sign(0)
-        sign(1)
-        ev_v(*d75(0))
-        if b == 0:
-            up(V.tensor_scalar(T.hi[:, 0:1], T.q31[:, 0:1], 16, -256.0, A.is_ge, A.mult), "wl")
-            up(V.tensor_scalar(T.wt[:, 0:1], T.q31[:, 0:1], -256, None, A.add), "wl")
-            ev_s(*d75(1))
-        else:
-            ev_v(*d75(1))
-        ev_s(*d75(2))
-        ev_s(*d75(3))
-        if b == 0:
-            eT(3)
-        wt("S", "ac0", "wl")
-        up(S.activation(ov[:, 0:1], T.cnt[:, 4 * b:4 * b + 1], F.Identity, bias=T.wt[:, 0:1], scale=T.lo[:, 0:1]), "ov")
-        wt("S", "ac1", "ov")
-        up(S.activation(ov[:, 1:2], T.cnt[:, 4 * b + 1:4 * b + 2], F.Identity, bias=ov[:, 0:1], scale=T.hi[:, 0:1]), "ov")
-        wt("S", "ov", "ucd")
-        up(S.activation(oa[:], T.uc[:], F.Abs, bias=ov[:, 1:2], scale=-1.0), "eq")
-        if b == 0:
-            for k in range(2):
-                fill(T.dp[:, 128 * k:128 * k + 128], -1024.0, "fp")
-            up(S.activation(T.mk[:, 2:3], T.lo[:, 0:1], F.Identity, bias=-1.0), "tb")
-            for k in range(3):
-                fill(MT[:, 128 * k:128 * k + 128], 0.0, "zm")
-            wt("S", "tb")
-            up(S.activation(T.tb[:], T.uc[:], F.Identity, bias=T.mk[:, 2:3], scale=-1.0 / 256), "tb")
+            pick_z(2, 0)
+            pick_z(2, 1)
         wt("V", "ac0", "ac1")
         up(V.tensor_copy(OF[:, 0:2], T.cnt[:, 4 * b:4 * b + 2]), "cv")
         wt("g", *(("cv",) if b else ("ac0", "ac1")))
-        hl = h1 if b else h0
-        rid, pid = topo.addr(hl, core)
-        e = topo.engines(core, hl)
-        g.remote_dma(T["hl%d" % b if b else "hf"][:], OF[:] if b else T.cnt[:, 0:2], T.sem["hl%d" % b], T.sem["loc"], pid, rid, bits(e))
-        due("loc", len(e))
+        write(h1 if b else h0, el, "hl%d" % b, OF[:] if b else T.cnt[:, 0:2], T["hl%d" % b if b else "hf"][:])
 
         for k in range(4):
-            new(k)
-        wt("V", "ga", "zn")
+            wt("V", "f%d" % k, "e%d" % k, "cv")
+            up(V.tensor_tensor(NT[:, 384 + k:512:4], D75[:, 128 * k:128 * k + 128].indirect(OF[:, 0:2]),
+                               T.dtk[:, 96 * k + 32 * b:96 * k + 32 * b + 32], A.add), "ga")
+        for h in range(2):
+            wt("V", "o%d" % h)
+            turn(ot, oa, h, "vl")
+        wt("V", "ga")
         up(V.quantize_mx(KC[:, 0:128], KS[:, 0:128], NT[:]), "qn")
         wt("g", "qn")
-        ec, ez = parts(topo.engines(core, h0))
-        g.remote_dma_fused([
-            send(h0, ec, "hc%d" % b, KC[:, 96:128].bitcast(dt.uint8), T["hc%d" % b][:, 0:32].bitcast(dt.uint8)),
-            send(h1, ez, "hz%d" % b, KS[:, 0:128], T["hz%d" % b][:, 0:128])], local_sem=T.sem["loc"])
+        sends = [(h0, ec, "hc%d" % b, KC[:, 96:128].bitcast(dt.uint8), T["hc%d" % b][:].bitcast(dt.uint8)),
+                 (h1, ez, "hz%d" % b, KS[:, 96:128], T["hz%d" % b][:])]
+        for a in (sends if b else sends[::-1]):
+            write(*a)
 
         step = stepper("vl")
         if b == 0:
-            wt("V", "io", "fl")
-            up(V.tensor_tensor(T.du[:, 0:256:32], T.q15[:], T.k8[:], A.add), "c8")
-            up(V.memset(T.mk[:, 0:1], 1024.0), "mk")
-        step(lambda: V.transpose(ot[:], oa[:]), "eq")
-        if b == 0:
-            wt("V", "c8")
-            up(V.tensor_scalar(T.cf[:], T.du[:, 0:256:32], -224.0, None, A.add), "c8")
-            for k in (1, 2):
-                up(V.tensor_scalar(T.lx[:, 16 * k:16 * k + 16], T.lx[:, 0:16], 32 * k - 96, None, A.add), "lx")
-        wt("V", "vl", "c8")
-        first(om, T.du, ot, "vl")
-        if b == 0:
             wt("V", "ldx", "xt")
             up(V.quantize_mx(T.xqc[:], T.xqs[:], T.xs[:]), "qx")
-            up(V.tensor_scalar(T.mk[:, 1:2], T.lo[:, 0:1], 3.0, 512.0, A.mult, A.add), "mk")
-        if b == 2:
+            wt("E", "sc0", "sc1", "qx")
+            for k in range(4):
+                mx(px[k][:, 0:128], *hb(k), T.xqc[:], T.xqs[:], "t%d" % k)
+        step(lambda: V.tensor_tensor_scan(om[:], T.du[:], ot[:], -4.0, A.max, A.min), "c8")
+        if last:
             wt("V", "ldw")
             up(V.quantize_mx(T.wqc[:], T.wqs[:], T.ws[:]), "qw")
+        else:
+            pick_c(b + 1, 0)
         wt("V", "vl")
-        for k in range(2):
-            up(V.tensor_copy(LA[:, k:8:2], om[:, 128 * k + 31:128 * k + 128:32]), "vl")
-        up(V.tensor_scalar(w[:], om[:, 31:256:32], 32.0, 32.0, A.is_ge, A.mult), "oc")
-        wt("V", "vl", "qn")
-        wt("S", "vl", "qn")
-        up(V.tensor_copy(WC[:, 160:288].bitcast(dt.uint32), KC[:, 96:256].bitcast(dt.uint32).indirect(LA[:])), "pa")
-        up(S.activation(WS[:, 160:288], KS[:, 96:256].indirect(LA[:]), F.Copy), "pz")
-        wt("V", "oc", "vp", "fp")
-        up(V.tensor_tensor(T.dp[:, 0:256:32], T.cf[:], w[:], A.subtract), "dp")
-        if b == 1:
-            pick_z(2, 0)
+        up(V.tensor_scalar(LA[:], om[:, 31:256:32], 256.0, None, A.mult), "la")
+        up(V.tensor_scalar(w[:], om[:, 31:256:32], 0.125, -160.0, A.is_ge, A.mult), "oc")
+        wt("V", "qn", "la")
+        wt("S", "qn", "la")
+        up(V.tensor_copy(WC[:, 128:256].bitcast(dt.uint32), KC[:, 96:256].bitcast(dt.uint32).indirect(LA[:])), "pa")
+        up(S.activation(WS[:, 128:256], KS[:, 96:256].indirect(LA[:]), F.Copy), "pz")
+        wt("V", "io", "fp", "vp", "oc")
+        up(V.tensor_tensor(T.dp[:, 31:256:32], T.cf[:], w[:], A.add), "dp")
         if b == 0:
             for k in range(4):
-                wt("E", "qx", "e%d" % k)
-                mx(pd[k][:, 0:128], *hb(k), T.xqc[:], T.xqs[:], "t%d" % k)
-                ev_s(T.dtk[:, 96 * k + 32:96 * k + 96], pd[k][:, 32:96], "t%d" % k, "f%d" % k, 0.5)
-            pick_c(1, 0, 2)
-            pick_c(2, 0)
-            pick_z(1, 0, 2)
+                ev_s(T.dtk[:, 96 * k + 32:96 * k + 96], px[k][:, 32:96], "t%d" % k, "f%d" % k, 0.5)
+            pick_c(1, 1)
+            up(V.quantize_mx(WC[:, 288:416], WS[:, 288:416], T.kbs[:]), "g2")
+            wt("E", *four("e"), "pa", "pz")
+            for k in range(4):
+                mx(pd[k][:, 0:128], *hb(k), WC[:, 128:256], WS[:, 128:256], "a%d" % k)
+                (ev_s if k % 2 else ev_v)(T.da[:, 128 * k:128 * k + 128], pd[k][:, 0:128], "a%d" % k, "da", 1.0)
+            for h in range(2):
+                pick_z(1, h)
+            up(V.memset(MT[:, 0:384], 0.0), "zm")
+        if last:
+            wt("E", *four("e"), "g2", "g3", "qw")
+            later = [y_of(0, 288, 0, 128, ev_s)]
+            wt("E", "pa", "pz")
+            later.append(y_of(1, 128, 0, 128, ev_s))
 
         no = len(topo.engines(helpers(dst, core, T, topo)[0], core))
-        due("rl%d" % b, no)
+        for n in ("rl", "rc", "rz"):
+            due("%s%d" % (n, b), no)
         step = stepper("vp")
+        wt("E", "g2", "g3", "sc0", "sc1", *four("f"), *four("n"))
+        wt("V", "mk", "tp", "rl%d" % b)
+        for h in range(2):
+            up(V.tensor_scalar(pv[:, h:h + 1], (PL if b else T.pf)[:, h:h + 1], col(AHEAD + h), None, A.add), "p%d" % h)
         if b:
-            step(lambda: V.tensor_scalar(pv[:, 0:1], PL[:, 0:1], T.lo[:, 0:1], -256.0, A.mult, A.add), "rl%d" % b)
+            wt("V", "pa")
+            wt("S", "pz", "rl%d" % b)
+            up(V.tensor_copy(XC[:, 0:32].bitcast(dt.uint32), WC[:, 128:256].bitcast(dt.uint32).indirect(PL[:, 0:2])), "pc")
+            up(S.activation(XS[:, 0:32], WS[:, 128:256].indirect(PL[:, 0:2]), F.Copy), "ps")
+            wt("E", "pc", "ps")
+            for k in range(4):
+                mx(px[k][:, 0:128], *hb(k), XC[:, 0:128], XS[:, 0:128], "zd", True, False)
         else:
-            wt("V", "rl0", "mk")
             up(V.tensor_copy(PL[:], T.pf[:]), "pu")
-            step(lambda: V.tensor_tensor_scan(pv[:, 0:2], T.mk[:, 0:2], T.pf[:], 0.0, A.add, A.min))
-        wt("V", "pu", "pa", "zd", "t0", "t1", "t2", "t3", "xca0", "xcb0")
-        wt("S", "rl%d" % b, "pu", "pz", "zd", "xza0", "xzb0")
-        up(V.tensor_copy(T.zc[:, 0:32].bitcast(dt.uint32), WC[:, 160:288].bitcast(dt.uint32).indirect(PL[:, 0:2])), "pc")
-        up(S.activation(T.zs[:, 0:32], WS[:, 160:288].indirect(PL[:, 0:2]), F.Copy), "ps")
-        if b == 1:
-            pick_z(2, 1)
+            wt("S", "da", "pu")
+            for k in range(4):
+                up(S.activation(T.dz[:, 32 * k:32 * k + 32], T.da[:, 128 * k:128 * k + 128].indirect(PL[:, 0:2]), F.Copy), "z%d" % k)
+        for h in range(2):
+            wt("V", "p%d" % h)
+            up(V.tensor_scalar(pa[:, 128 * h:128 * h + 128], T.up[:, 128 * h:128 * h + 128], pv[:, h:h + 1], pv[:, h:h + 1],
+                               A.is_equal, A.mult), "p%d" % h)
+        if last:
+            for f in later:
+                f()
         wt("Y", "rl%d" % b, "ac0", "ac1")
         if b == 0:
             up(Y.dma_start(T.ws[:], T.w[:]), "ldw", 16)
         for h in range(2):
             up(Y.dma_start(T.ch[b:b + 1, 16 * h:16 * h + 16], T.cnt[0:16, 4 * b + h:4 * b + h + 1]), "st", 16)
-        wt("E", "pc", "ps", "sc0", "sc1", "f0", "f1", "f2", "f3", "n0", "n1", "n2", "n3")
-        for k in range(4):
-            mx(px[k][:, 0:128], *hb(k), T.zc[:], T.zs[:], "zd", True, False)
-        if b:
-            step(lambda: V.tensor_scalar(pv[:, 1:2], PL[:, 1:2], T.hi[:, 0:1], pv[:, 0:1], A.mult, A.add))
-        step(lambda: V.tensor_scalar(pa[:], (T.uc if b else T.tb)[:], pv[:, 1:2], T.wt[:, 0:1], A.is_equal, A.mult), "tb")
-        step(lambda: V.transpose(ptt[:], pa[:]))
-        wt("V", "vp", "dp")
-        first(pm, T.dp, ptt, "v0", "v1")
-        for k in range(2):
-            wt("V", "v%d" % k)
-            up(V.tensor_tensor(u[:, k:8:2], pm[:, 128 * k + 31:128 * k + 128:32], w[:, 4 * k:4 * k + 4], A.add), "vp")
-        step(lambda: V.tensor_scalar(LF[:], u[:], 256.0, None, A.add))
-
-        due("rc%d" % b, no)
-        due("rz%d" % b, no)
         wt("E", "rc%d" % b, "rz%d" % b)
-        wt("S", "qm", "zm")
         for k in range(4):
-            mx(px[k][:, 0:128], *hb(k), WC[:, 128:256], WS[:, 128:256], "m%d" % k, False, True)
-            wt("S", "m%d" % k)
-            up(S.activation(MT[:, 384 + k:512:4], px[k][:, 0:32], F.Copy), "n%d" % k)
-        wt("V", "n0", "n1", "n2", "n3")
-        up(V.quantize_mx(WC[:, 0:128], WS[:, 0:128], MT[:]), "qm")
-        wt("V", "qm", "vp")
-        wt("S", "qm", "vp")
-        oc, os = (T["kwc%d" % (b + 1)][:, 128:256], T["kws%d" % (b + 1)][:, 128:256]) if b + 1 < R else (T.fc[:], T.fs[:])
-        up(V.tensor_copy(oc.bitcast(dt.uint32), WC[:, 96:288].bitcast(dt.uint32).indirect(LF[:])), "pf")
-        up(S.activation(os, WS[:, 96:288].indirect(LF[:]), F.Copy), "pg")
+            mx(px[k][:, 0:128], *hb(k), WC[:, 256:384], WS[:, 256:384], "m%d" % k, b == 0, True)
 
-    wt("E", "pf", "pg", "qw", "n0")
-    mx(T.py[:, 0:128], T.wqc[:], T.wqs[:], T.fc[:], T.fs[:], "ym")
+        def add(k):
+            wt("V", "zm", "z%d" % k, "m%d" % k)
+            up(V.tensor_tensor(MT[:, 384 + k:512:4], px[k][:, 0:32], T.dz[:, 32 * k:32 * k + 32], A.add), "n%d" % k)
+
+        for h in range(2):
+            wt("V", "p%d" % h)
+            turn(pt, pa, h, "vp")
+        for k in range(0 if b else 1):
+            add(k)
+        step(lambda: V.tensor_tensor_scan(pm[:], pt[:], T.dp[:], 0.0, A.max, A.add), "dp")
+        for k in range(0 if b else 3):
+            add(1 + k)
+        if b == 1:
+            pick_c(2, 1)
+        step(lambda: V.tensor_scalar(LF[:], pm[:, 31:256:32], -1.0, col(END), A.mult, A.add))
+
+        wt("S", "qm")
+        for k in range(4 if b else 0):
+            ev_s(MT[:, 384 + k:512:4], px[k][:, 0:32], "m%d" % k, "n%d" % k, 1.0)
+        if last:
+            y_of(2, 256, 0, 32, ev_s)()
+        wt("V", *four("n"))
+        up(V.quantize_mx(WC[:, 0:128], WS[:, 0:128], MT[:]), "qm")
+        wt("V", "g2", "vp", "qm")
+        wt("S", "g2", "g3", "vp", "qm")
+        if last:
+            outs = [(T.fc[:], T.fs[:], "pf", "pg")]
+        else:
+            outs = [(T["kwc%d" % (b + 1)][:, 128:256], T["kws%d" % (b + 1)][:, 128:256], "pf", "pg"),
+                    (T["wc%d" % (b + 1)][:, 288:416], T["wsc%d" % (b + 1)][:, 288:416], "g2", "g3")]
+        for oc, os, sc, sz in outs:
+            up(V.tensor_copy(oc.bitcast(dt.uint32), WC[:, 96:416].bitcast(dt.uint32).indirect(LF[:])), sc)
+            up(S.activation(os, WS[:, 96:416].indirect(LF[:]), F.Copy), sz)
+
+    def scales(q, k):
+        up(q.dma_start(T.osc[4 * k:4 * k + 4, :], T.fs[32 * k:32 * k + 4, :]), "st", 16)
+
+    wt("E", "qm")
+    y_of(3, 0, 96, 32, ev_v)()
     wt("Y", "pf")
     up(Y.dma_start(T.oc[:], T.fc[:].bitcast(dt.uint8)), "st", 16)
-    wt("S", "pg")
-    for k in range(4):
-        up(S.dma_start(T.osc[4 * k:4 * k + 4, :], T.fs[32 * k:32 * k + 4, :]), "st", 16)
+    wt("Y", "pg")
+    scales(Y, 0)
+    scales(Y, 1)
     wt("V", "ym")
-    up(V.tensor_copy(T.ys[:], T.py[:, 0:128]), "ye")
-    wt("Y", "ye")
-    up(Y.dma_start(T.y[:], T.ys[:]), "st", 16)
+    wt("S", "pg", "ym")
+    up(V.tensor_copy(T.ys[:, 0:64], T.yw[:].indirect(LF[:, 0:4])), "ye")
+    up(S.activation(T.ys[:, 64:128], T.yw[:].indirect(LF[:, 4:8]), F.Copy), "ye")
+    wt("S", "ye")
+    up(S.dma_start(T.y[:], T.ys[:]), "st", 16)
+    scales(S, 2)
+    scales(S, 3)
     wt("Y", "st")
     for m in sorted(cnt):
         if max([seen.get((q, m), 0) for q in qn]) < cnt[m]:

from concourse.mybir import dt, AluOpType, ActivationFunctionType

R = 3
F8, U8, U16, BF, F32, I32 = "float8_e4m3fn_x4", "uint8", "uint16", "bfloat16", "float32", "int32"


def sb(n, d):
    return ("sbuf", [128, n], d)


SCRATCH = {
    "kbs": sb(512, BF), "xs": sb(512, BF), "ws": sb(512, BF), "zh": sb(128, BF), "zf": sb(516, BF),
    "hbc": sb(512, F8), "hbs": sb(512, U8), "iq": sb(8, I32), "q15": sb(12, I32), "k8": sb(8, F32), "cf": sb(8, F32),
    "lx": sb(16, U16), "cc": sb(12, F32), "hf": sb(2, F32), "pf": sb(2, F32), "uc": sb(128, BF), "uo": sb(256, F32), "up": sb(256, BF),
    "xqc": sb(128, F8), "xqs": sb(128, U8), "wqc": sb(128, F8), "wqs": sb(128, U8), "dtk": sb(384, BF),
    "fc": sb(128, F8), "fs": sb(128, U8), "ys": sb(128, F32), "yw": sb(320, F32),
    "scn": sb(768, F32), "jnk": sb(768, BF), "cnt": sb(12, F32), "nt": sb(512, BF), "mt": sb(512, BF),
    "da": sb(512, BF), "dz": sb(128, BF), "du": sb(256, BF), "dp": sb(256, BF),
}
for _n in ("ps0", "ps1", "py", "pe", "pd0", "pd1", "pd2", "pd3"):
    SCRATCH[_n] = ("psum", [128, 512], F32)
for _b in range(R):
    for _n, _w, _d in (("xrc", 256, F8), ("xrs", 256, U8), ("kwc", 256, F8), ("kws", 256, U8), ("wc", 416, F8), ("wsc", 416, U8),
                       ("d75_", 512, BF), ("of", 2, U16), ("pl", 2, U16), ("la", 8, U16), ("lf", 8, U16),
                       ("hl", 2, U16), ("hc", 32, F8), ("hz", 32, U8), ("pv", 2, F32), ("ow", 8, F32),
                       ("oa", 256, BF), ("ot", 256, BF), ("om", 256, BF), ("pa", 256, BF), ("pt", 256, BF), ("pm", 256, BF)):
        SCRATCH["%s%d" % (_n, _b)] = sb(_w, _d)

SEMAPHORES = ["ms", "mz", "tb", "pu", "zm", "fp", "xt", "zn", "lx", "wl", "ldk", "ld0", "ldx", "ldw", "io", "zfd", "cs", "c8",
              "qk", "q0", "qx", "qw", "s0", "s1", "sc0", "sc1", "ac0", "ac1", "cv", "ga", "qn", "vl", "vp", "la", "cf", "sg", "mk", "oc",
              "fl", "dp", "pa", "pz", "pc", "ps", "zd", "qm", "pf", "pg", "ym", "ye", "st", "loc", "ucd", "iq", "g2", "g3", "da",
              "o0", "o1", "p0", "p1", "tp"]
for _b in range(4):
    SEMAPHORES += ["%s%d" % (_n, _b) for _n in ("hb", "d", "e", "t", "f", "m", "n", "a", "z", "y")]
for _b in range(R):
    SEMAPHORES += ["%s%d" % (_n, _b) for _n in ("hl", "hc", "hz", "rl", "rc", "rz", "xca", "xcb", "xza", "xzb")]

FIRST = "k0 q0 h0 c0 z0 z1 k1 q1 c1 h1 h2 s0 s1 G0 G1 G2 n0 n1 h3 G3 g0 g1 v0 v1 a2 o0 a3 o1"
LATER = "s0 s1 G0 G1 G2 G3 n0 n1 g0 g1 v0 v1 a2 o0 a3 o1"
LANE, SLOT, SIGN, PART, END, BACK, OWN, AHEAD = 0, 1, 2, 3, 4, 6, 8, 10


def helpers(core, dst, T, topo):
    c = [h for h in topo.cores_of(core) if T.rank_of(h) is None and topo.die(h) == topo.die(core) and topo.may_write(h, dst)]
    return c[0], c[-1]


def bits(engines):
    return sum(1 << e for e in engines)


def lanes(engines, b):
    n = len(engines) // 2
    return (engines, engines, engines) if b else (engines[:n], engines[:n], engines[n:])


def hand_on(g, core, T, topo):
    home = [c for c in topo.cores_of(core) if T.rank_of(c) is not None]
    if not home:
        return
    r, sent = T.rank_of(home[0]), 0
    for b in range(R):
        dst = T.cores[r ^ (1 << b)]
        ha, hb = helpers(home[0], dst, T, topo)
        if core not in (ha, hb):
            continue
        rid, pid = topo.addr(dst, core)
        eng = topo.engines(core, dst)
        el, ez, ec = lanes(topo.engines(home[0], core), b)
        if core == (hb if b else ha):
            g.wait_ge(T.sem["hl%d" % b], len(el))
            g.remote_dma(T["pl%d" % b if b else "pf"][:], T["hl%d" % b if b else "hf"][:], T.sem["rl%d" % b], T.sem["loc"], pid, rid, bits(eng))
            sent += len(eng)
        if core == ha:
            g.wait_ge(T.sem["hc%d" % b], len(ec))
            g.remote_dma(T["wc%d" % b][:, 256:288].bitcast(dt.uint8), T["hc%d" % b][:].bitcast(dt.uint8),
                         T.sem["rc%d" % b], T.sem["loc"], pid, rid, bits(eng))
        else:
            g.wait_ge(T.sem["hz%d" % b], len(ez))
            g.remote_dma(T["wsc%d" % b][:, 256:288], T["hz%d" % b][:], T.sem["rz%d" % b], T.sem["loc"], pid, rid, bits(eng))
        sent += len(eng)
    if sent:
        g.wait_ge(T.sem["loc"], sent)


def rank_program(g, core, T, topo):
    rank = T.rank_of(core)
    if rank is None:
        hand_on(g, core, T, topo)
        return
    A, F = AluOpType, ActivationFunctionType
    V, S, E, Y = g.vector, g.scalar, g.tensor, g.sync
    cnt, seen, qn = {}, {}, {"V": V, "S": S, "E": E, "Y": Y, "g": g}

    def up(ins, name, n=1):
        ins.then_inc(T.sem[name], n)
        cnt[name] = cnt.get(name, 0) + n

    def wt(q, *names):
        for m in names:
            if cnt.get(m, 0) > seen.get((q, m), 0):
                qn[q].wait_ge(T.sem[m], cnt[m])
                seen[(q, m)] = cnt[m]

    def due(name, n):
        cnt[name] = cnt.get(name, 0) + n

    def four(n):
        return ["%s%d" % (n, k) for k in range(4)]

    def mx(out, lc, ls, rc, rs, name, start=True, stop=True):
        up(E.matmul_mx(out, lc, ls, rc, rs, start, stop), name)

    def hb(b):
        return T.hbc[:, 128 * b:128 * b + 128], T.hbs[:, 128 * b:128 * b + 128]

    def make_hb(b):
        wt("V", "zfd", "mz")
        up(V.quantize_mx(*hb(b), T.zf[:, 3 - b:515 - b]), "hb%d" % b)

    def write(h, e, sem, src, dst):
        rid, pid = topo.addr(h, core)
        due("loc", len(e))
        g.remote_dma(dst, src, T.sem[sem], T.sem["loc"], pid, rid, bits(e))

    def fill(out, c, name):
        up(S.activation(out, T.zh[:], F.Copy, scale=2.0 * c), name)

    def col(j):
        return T.cc[:, j:j + 1]

    def const(j, i, scale, bias, name):
        up(S.activation(col(j), col(i), F.Identity, bias=bias, scale=scale), name)

    pd = [T["pd%d" % b] for b in range(4)]
    px = [T.py, T.pe, T.ps0, T.ps1]
    NT, MT = T.nt, T.mt

    up(Y.dma_start(NT[:, 384:512], T.x[:, 0:128]), "ld0", 16)
    up(Y.dma_start(T.kbs[:], T.kb[:]), "ldk", 16)
    wt("Y", "ld0")
    up(Y.dma_start(T.xs[:, 128:384], T.x[:, 128:384]), "ldx", 16)
    up(g.iota(T.iq[:], [[0, 8]], 0, 1), "iq")
    up(V.memset(T.zh[:], 0.5), "ms")
    for k in range(3):
        up(V.memset(T.zf[:, k:516:4], 0.0), "mz")
    up(V.memset(T.zf[:, 515:516], 0.0), "mz")
    wt("g", "ms")
    up(g.affine_select(T.zf[:, 3:515:4], T.zh[:], [[-1, 128]], A.is_equal, 0.0, 0, 1), "zfd")
    up(g.iota(T.uc[:], [[32, 4], [0, 2], [1, 16]], 8, 0, allow_small_or_imprecise_dtypes=True), "ucd")
    up(g.iota(T.k8[:], [[16, 8]], 32, 0, allow_small_or_imprecise_dtypes=True), "io")
    up(g.iota(T.cf[:], [[-16, 8]], -48, 0, allow_small_or_imprecise_dtypes=True), "io")
    wt("S", "ms")
    for k in range(3):
        fill(NT[:, 128 * k:128 * k + 128], 0.0, "zn")
    fill(T.xs[:, 0:128], 0.0, "xt")
    fill(T.xs[:, 384:512], 0.0, "xt")
    wt("V", "iq")
    up(V.tensor_scalar(T.q15[:, 0:8], T.iq[:], 15, None, A.bitwise_and), "cs")
    up(V.tensor_scalar(T.q15[:, 8:9], T.iq[:, 0:1], 31, None, A.bitwise_and), "cs")
    wt("V", "cs")
    up(V.tensor_copy(T.cc[:, LANE:SLOT + 1], T.q15[:, 7:9]), "cf")
    for h in range(2):
        up(V.tensor_scalar(T.lx[:, 8 * h:8 * h + 8], T.q15[:, 0:8], 16 * h, None, A.add), "lx")

    def pick_c(b, h):
        wt("V", "qx" if b else "q0", "lx")
        src = T.xqc[:, 32 * b:32 * b + 32] if b else T.kwc0[:, 96:128]
        up(V.tensor_copy(T["xrc%d" % b][:, 128 * h:128 * h + 128].bitcast(dt.uint32),
                         src.bitcast(dt.uint32).indirect(T.lx[:, 8 * h:8 * h + 8])), "xc%s%d" % ("ab"[h], b))

    def pick_z(b, h):
        wt("S", "qx" if b else "q0", "lx")
        src = T.xqs[:, 32 * b:32 * b + 32] if b else T.kws0[:, 96:128]
        up(S.activation(T["xrs%d" % b][:, 128 * h:128 * h + 128], src.indirect(T.lx[:, 8 * h:8 * h + 8]), F.Copy), "xz%s%d" % ("ab"[h], b))

    def ev_v(out, src, d, e, scale):
        wt("V", d)
        up(V.tensor_scalar(out, src, scale, None, A.mult), e)

    def ev_s(out, src, d, e, scale):
        wt("S", d)
        up(S.activation(out, src, F.Copy, scale=scale), e)

    def quantise(k):
        wt("V", *(("ldk",) if k else ("ld0", "zn")))
        up(V.quantize_mx(T.kwc0[:, 128 * k:128 * k + 128], T.kws0[:, 128 * k:128 * k + 128], (T.kbs if k else NT)[:]), "qk" if k else "q0")

    def lists(k):
        if k == 0:
            wt("S", "cf")
            up(S.activation(col(SIGN), col(SLOT), F.Sign, bias=-15.5), "sg")
            for h in range(2):
                const(BACK + h, LANE, -1.0 / 256, -h / 16.0, "sg")
        elif k == 1:
            wt("S", "sg")
            for h in range(2):
                const(OWN + h, SIGN, 8.0, col(BACK + h), "wl")
            wt("S", "ucd", "wl")
            for h in range(2):
                up(S.activation(T.uo[:, 128 * h:128 * h + 128], T.uc[:], F.Identity, bias=col(OWN + h)), "tb")
        else:
            const(PART, LANE, 1.0 / 256, 0.0, "fl")
            for h in range(2):
                fill(T.du[:, 128 * h:128 * h + 128], -4.0, "fl")
            for h in range(2):
                const(AHEAD + h, LANE, -1.0, 32.0 - 16 * h, "mk")
            const(END, LANE, 1.0, -16.0, "mk")
            wt("S", "io", "fl")
            up(S.activation(T.du[:, 0:256:32], T.k8[:], F.Identity, bias=col(PART), scale=1.0 / 256), "c8")
            wt("S", "mk")
            for h in range(2):
                const(BACK + h, SIGN, 8.0, col(AHEAD + h), "wl")
            for h in range(2):
                fill(T.dp[:, 128 * h:128 * h + 128], 0.0, "fp")
            wt("S", "wl")
            for h in range(2):
                up(S.activation(T.up[:, 128 * h:128 * h + 128], T.uc[:], F.Identity, bias=col(BACK + h)), "tp")

    def stepper(chain):
        def step(f, *names):
            wt("V", *names, chain)
            up(f(), chain)
        return step

    for b in range(R):
        KC, KS, WC, WS = (T["%s%d" % (n, b)] for n in ("kwc", "kws", "wc", "wsc"))
        XC, XS, D75 = (T["%s%d" % (n, b)] for n in ("xrc", "xrs", "d75_"))
        OF, PL, LA, LF, pv, w = (T["%s%d" % (n, b)] for n in ("of", "pl", "la", "lf", "pv", "ow"))
        oa, ot, om, pa, pt, pm = (T["%s%d" % (n, b)] for n in ("oa", "ot", "om", "pa", "pt", "pm"))
        dst = T.cores[rank ^ (1 << b)]
        h0, h1 = helpers(core, dst, T, topo)
        el, ez, ec = lanes(topo.engines(core, h0), b)
        last = b + 1 == R

        def dG(k):
            c = 128 if b else 96
            wt("E", "qk", "pf", "pg", "e%d" % k, "hb%d" % k, "da")
            mx(pd[k][:, 0:256 - c], *hb(k), KC[:, c:256], KS[:, c:256], "d%d" % k)

        def score(h):
            wt("E", "sc%d" % h, "n%d" % (2 + h), "xc%s%d" % ("ab"[h], b), "xz%s%d" % ("ab"[h], b), "qk", "pf", "pg")
            mx(T["ps%d" % h][:, 0:128], XC[:, 128 * h:128 * h + 128], XS[:, 128 * h:128 * h + 128], KC[:, 128:256], KS[:, 128:256], "s%d" % h)

        def d75(k, ev):
            c = 0 if b else 32
            ev(D75[:, 128 * k:128 * k + 128], pd[k][:, c:c + 128], "d%d" % k, "e%d" % k, 1.5)
            if b == 0:
                ev(T.dtk[:, 96 * k:96 * k + 32], pd[k][:, 0:32], "d%d" % k, "e%d" % k, 0.5)

        def sign(h):
            j = 2 * b + h
            wt("S", "sc%d" % h)
            up(S.activation(T.jnk[:, 128 * j:128 * j + 128], T.scn[:, 128 * j:128 * j + 128], F.Sign,
                            bias=T.scn[:, 128 * j + 127:128 * j + 128], scale=-1.0, accum_out=T.cnt[:, 4 * b + h:4 * b + h + 1]), "ac%d" % h)

        def scan(h):
            j = 2 * b + h
            wt("V", "zn", "s%d" % h)
            up(V.tensor_tensor_scan(T.scn[:, 128 * j:128 * j + 128], T["ps%d" % h][:, 0:128], NT[:, 0:128], -1e29, A.max, A.add), "sc%d" % h)

        def own(h):
            wt("S", "tb", "ac%d" % h)
            up(S.activation(oa[:, 128 * h:128 * h + 128], T.uo[:, 128 * h:128 * h + 128], F.Abs,
                            bias=T.cnt[:, 4 * b + h:4 * b + h + 1], scale=-1.0), "o%d" % h)

        def turn(t, a, h, name):
            up(V.transpose(t[:, h:256:2], a[:, 128 * h:128 * h + 128]), name)

        def y_of(k, c, lo, n, ev):
            mx(pd[k][:, 0:128], T.wqc[:], T.wqs[:], WC[:, c:c + 128], WS[:, c:c + 128], "y%d" % k)
            return lambda: ev(T.yw[:, c + lo - 96:c + lo - 96 + n], pd[k][:, lo:lo + n], "y%d" % k, "ym", 1.0)

        act = {"h": make_hb, "q": quantise, "c": lambda k: pick_c(0, k), "z": lambda k: pick_z(0, k), "k": lists,
               "s": score, "G": dG, "n": scan, "g": sign, "v": lambda k: d75(k, ev_v), "a": lambda k: d75(k, ev_s), "o": own}
        for a in (LATER if b else FIRST).split():
            act[a[0]](int(a[1]))
        if b == 0:
            lists(2)
        if b == 1:
            pick_z(2, 0)
            pick_z(2, 1)
        wt("V", "ac0", "ac1")
        up(V.tensor_copy(OF[:, 0:2], T.cnt[:, 4 * b:4 * b + 2]), "cv")
        wt("g", *(("cv",) if b else ("ac0", "ac1")))
        write(h1 if b else h0, el, "hl%d" % b, OF[:] if b else T.cnt[:, 0:2], T["hl%d" % b if b else "hf"][:])

        for k in range(4):
            wt("V", "f%d" % k, "e%d" % k, "cv")
            up(V.tensor_tensor(NT[:, 384 + k:512:4], D75[:, 128 * k:128 * k + 128].indirect(OF[:, 0:2]),
                               T.dtk[:, 96 * k + 32 * b:96 * k + 32 * b + 32], A.add), "ga")
        for h in range(2):
            wt("V", "o%d" % h)
            turn(ot, oa, h, "vl")
        wt("V", "ga")
        up(V.quantize_mx(KC[:, 0:128], KS[:, 0:128], NT[:]), "qn")
        wt("g", "qn")
        sends = [(h0, ec, "hc%d" % b, KC[:, 96:128].bitcast(dt.uint8), T["hc%d" % b][:].bitcast(dt.uint8)),
                 (h1, ez, "hz%d" % b, KS[:, 96:128], T["hz%d" % b][:])]
        for a in (sends if b else sends[::-1]):
            write(*a)

        step = stepper("vl")
        if b == 0:
            wt("V", "ldx", "xt")
            up(V.quantize_mx(T.xqc[:], T.xqs[:], T.xs[:]), "qx")
            wt("E", "sc0", "sc1", "qx")
            for k in range(4):
                mx(px[k][:, 0:128], *hb(k), T.xqc[:], T.xqs[:], "t%d" % k)
        step(lambda: V.tensor_tensor_scan(om[:], T.du[:], ot[:], -4.0, A.max, A.min), "c8")
        if last:
            wt("V", "ldw")
            up(V.quantize_mx(T.wqc[:], T.wqs[:], T.ws[:]), "qw")
        else:
            pick_c(b + 1, 0)
        wt("V", "vl")
        up(V.tensor_scalar(LA[:], om[:, 31:256:32], 256.0, None, A.mult), "la")
        up(V.tensor_scalar(w[:], om[:, 31:256:32], 0.125, -160.0, A.is_ge, A.mult), "oc")
        wt("V", "qn", "la")
        wt("S", "qn", "la")
        up(V.tensor_copy(WC[:, 128:256].bitcast(dt.uint32), KC[:, 96:256].bitcast(dt.uint32).indirect(LA[:])), "pa")
        up(S.activation(WS[:, 128:256], KS[:, 96:256].indirect(LA[:]), F.Copy), "pz")
        wt("V", "io", "fp", "vp", "oc")
        up(V.tensor_tensor(T.dp[:, 31:256:32], T.cf[:], w[:], A.add), "dp")
        if b == 0:
            for k in range(4):
                ev_s(T.dtk[:, 96 * k + 32:96 * k + 96], px[k][:, 32:96], "t%d" % k, "f%d" % k, 0.5)
            pick_c(1, 1)
            up(V.quantize_mx(WC[:, 288:416], WS[:, 288:416], T.kbs[:]), "g2")
            wt("E", *four("e"), "pa", "pz")
            for k in range(4):
                mx(pd[k][:, 0:128], *hb(k), WC[:, 128:256], WS[:, 128:256], "a%d" % k)
                (ev_s if k % 2 else ev_v)(T.da[:, 128 * k:128 * k + 128], pd[k][:, 0:128], "a%d" % k, "da", 1.0)
            for h in range(2):
                pick_z(1, h)
            up(V.memset(MT[:, 0:384], 0.0), "zm")
        if last:
            wt("E", *four("e"), "g2", "g3", "qw")
            later = [y_of(0, 288, 0, 128, ev_s)]
            wt("E", "pa", "pz")
            later.append(y_of(1, 128, 0, 128, ev_s))

        no = len(topo.engines(helpers(dst, core, T, topo)[0], core))
        for n in ("rl", "rc", "rz"):
            due("%s%d" % (n, b), no)
        step = stepper("vp")
        wt("E", "g2", "g3", "sc0", "sc1", *four("f"), *four("n"))
        wt("V", "mk", "tp", "rl%d" % b)
        for h in range(2):
            up(V.tensor_scalar(pv[:, h:h + 1], (PL if b else T.pf)[:, h:h + 1], col(AHEAD + h), None, A.add), "p%d" % h)
        if b:
            wt("V", "pa")
            wt("S", "pz", "rl%d" % b)
            up(V.tensor_copy(XC[:, 0:32].bitcast(dt.uint32), WC[:, 128:256].bitcast(dt.uint32).indirect(PL[:, 0:2])), "pc")
            up(S.activation(XS[:, 0:32], WS[:, 128:256].indirect(PL[:, 0:2]), F.Copy), "ps")
            wt("E", "pc", "ps")
            for k in range(4):
                mx(px[k][:, 0:128], *hb(k), XC[:, 0:128], XS[:, 0:128], "zd", True, False)
        else:
            up(V.tensor_copy(PL[:], T.pf[:]), "pu")
            wt("S", "da", "pu")
            for k in range(4):
                up(S.activation(T.dz[:, 32 * k:32 * k + 32], T.da[:, 128 * k:128 * k + 128].indirect(PL[:, 0:2]), F.Copy), "z%d" % k)
        for h in range(2):
            wt("V", "p%d" % h)
            up(V.tensor_scalar(pa[:, 128 * h:128 * h + 128], T.up[:, 128 * h:128 * h + 128], pv[:, h:h + 1], pv[:, h:h + 1],
                               A.is_equal, A.mult), "p%d" % h)
        if last:
            for f in later:
                f()
        wt("Y", "rl%d" % b, "ac0", "ac1")
        if b == 0:
            up(Y.dma_start(T.ws[:], T.w[:]), "ldw", 16)
        for h in range(2):
            up(Y.dma_start(T.ch[b:b + 1, 16 * h:16 * h + 16], T.cnt[0:16, 4 * b + h:4 * b + h + 1]), "st", 16)
        wt("E", "rc%d" % b, "rz%d" % b)
        for k in range(4):
            mx(px[k][:, 0:128], *hb(k), WC[:, 256:384], WS[:, 256:384], "m%d" % k, b == 0, True)

        def add(k):
            wt("V", "zm", "z%d" % k, "m%d" % k)
            up(V.tensor_tensor(MT[:, 384 + k:512:4], px[k][:, 0:32], T.dz[:, 32 * k:32 * k + 32], A.add), "n%d" % k)

        for h in range(2):
            wt("V", "p%d" % h)
            turn(pt, pa, h, "vp")
        for k in range(0 if b else 1):
            add(k)
        step(lambda: V.tensor_tensor_scan(pm[:], pt[:], T.dp[:], 0.0, A.max, A.add), "dp")
        for k in range(0 if b else 3):
            add(1 + k)
        if b == 1:
            pick_c(2, 1)
        step(lambda: V.tensor_scalar(LF[:], pm[:, 31:256:32], -1.0, col(END), A.mult, A.add))

        wt("S", "qm")
        for k in range(4 if b else 0):
            ev_s(MT[:, 384 + k:512:4], px[k][:, 0:32], "m%d" % k, "n%d" % k, 1.0)
        if last:
            y_of(2, 256, 0, 32, ev_s)()
        wt("V", *four("n"))
        up(V.quantize_mx(WC[:, 0:128], WS[:, 0:128], MT[:]), "qm")
        wt("V", "g2", "vp", "qm")
        wt("S", "g2", "g3", "vp", "qm")
        if last:
            outs = [(T.fc[:], T.fs[:], "pf", "pg")]
        else:
            outs = [(T["kwc%d" % (b + 1)][:, 128:256], T["kws%d" % (b + 1)][:, 128:256], "pf", "pg"),
                    (T["wc%d" % (b + 1)][:, 288:416], T["wsc%d" % (b + 1)][:, 288:416], "g2", "g3")]
        for oc, os, sc, sz in outs:
            up(V.tensor_copy(oc.bitcast(dt.uint32), WC[:, 96:416].bitcast(dt.uint32).indirect(LF[:])), sc)
            up(S.activation(os, WS[:, 96:416].indirect(LF[:]), F.Copy), sz)

    def scales(q, k):
        up(q.dma_start(T.osc[4 * k:4 * k + 4, :], T.fs[32 * k:32 * k + 4, :]), "st", 16)

    wt("E", "qm")
    y_of(3, 0, 96, 32, ev_v)()
    wt("Y", "pf")
    up(Y.dma_start(T.oc[:], T.fc[:].bitcast(dt.uint8)), "st", 16)
    wt("Y", "pg")
    scales(Y, 0)
    scales(Y, 1)
    wt("V", "ym")
    wt("S", "pg", "ym")
    up(V.tensor_copy(T.ys[:, 0:64], T.yw[:].indirect(LF[:, 0:4])), "ye")
    up(S.activation(T.ys[:, 64:128], T.yw[:].indirect(LF[:, 4:8]), F.Copy), "ye")
    wt("S", "ye")
    up(S.dma_start(T.y[:], T.ys[:]), "st", 16)
    scales(S, 2)
    scales(S, 3)
    wt("Y", "st")
    for m in sorted(cnt):
        if max([seen.get((q, m), 0) for q in qn]) < cnt[m]:
            wt("g", m)
